import numpy as np
import ml_dtypes


def mxq(x, axis, fmt="e4m3"):
    dtype, down = {"e4m3": (ml_dtypes.float8_e4m3fn, 7), "e5m2": (ml_dtypes.float8_e5m2, 14)}[fmt]
    v = np.moveaxis(np.asarray(x, np.float32).astype(ml_dtypes.bfloat16).astype(np.float64), axis, -1)
    blocks = v.reshape(v.shape[:-1] + (-1, 32))
    amax = np.abs(blocks).max(-1, keepdims=True)
    byte = np.maximum(np.where(amax > 0, np.frexp(amax)[1] - 1 + 127, 0) - down, 1)
    scale = np.exp2(byte - 127.0)
    codes = (blocks / scale).astype(np.float32).astype(dtype).astype(np.float64)
    return np.moveaxis((codes * scale).reshape(v.shape), -1, axis)


WIDE = False


def mx_kscale(k):
    if not WIDE:
        return np.ones(k)
    levels = np.array([18, -18])
    if k % 512:
        return np.exp2(np.random.permutation(np.resize(levels, k // 32))).repeat(32)
    a = np.empty((k // 512, 16))
    for p in range(k // 512):
        a[p, :8] = np.random.permutation(np.resize(levels, 8))
        for g in range(8):
            far = levels[np.abs(levels - a[p, g]) >= 10]
            a[p, g + 8] = far[np.random.randint(len(far))]
    return np.exp2(a.ravel()).repeat(32)


def f64(x):
    return np.asarray(x).astype(np.float64)


def striped(idx):
    return np.tile(np.asarray(idx).reshape(-1, 16).T, (8, 1)).astype(np.uint16)


def unstriped(offs):
    return offs[:16].T.reshape(-1).astype(np.int64)


B, N, T, D, R = 1, 512, 2048, 512, 1024
LR = 0.1
EPS = 0.001


def setup_inputs():
    n = np.random.standard_normal
    idx = np.random.permutation(T)[:B * N]
    s = mx_kscale(D)[:, None]
    z = mx_kscale(R)[:, None]
    x = n((B, D, R))
    return {
        "xT": (x * s).astype(np.float32),
        "wT": (n((D, T)) * (1.00 / np.sqrt(D)) / s).astype(np.float32),
        "y": n((B, R, N)).astype(np.float32),
        "wt": (np.random.uniform(0.5, 1.5, (B, R, 1)) * 1.0 / np.sqrt(R) * z).astype(np.float32),
        "xm": (x.transpose(0, 2, 1) / z).astype(np.float32),
        "vT": (np.random.uniform(0.1, 0.5, (D, T))).astype(np.float32),
        "offs": striped(idx),
    }


def reference(xT, wT, y, wt, xm, vT, offs):
    idx = unstriped(offs)
    pick = lambda x: x[:, idx].reshape(x.shape[0], B, N).transpose(1, 0, 2)
    a = mxq(f64(xT), 1, "e4m3").transpose(0, 2, 1) @ mxq(pick(f64(wT)), 1, "e4m3")
    g = f64(wt) * np.minimum(np.maximum(a - f64(y), -1.0), 1.0)
    dw = mxq(f64(xm), 1, "e4m3").transpose(0, 2, 1) @ mxq(g, 1, "e5m2")
    nv = pick(f64(vT)) + dw * dw
    nw = -LR * dw / (np.sqrt(nv) + EPS)
    tables = []
    for old, new in ((wT, nw), (vT, nv),):
        table = f64(old) if old is not wT else np.zeros((D, T))
        table[:, idx] = new.transpose(1, 0, 2).reshape(D, B * N)
        tables.append(table)
    return tuple(tables)

@@ -1,0 +1,167 @@
+from contextlib import ExitStack
+
+import concourse.mybir as mybir
+
+N, T, D, R = 512, 2048, 512, 1024
+LR = 0.1
+EPS = 0.001
+FLOPS = 2 * 2 * D * R * N
+
+F32 = mybir.dt.float32
+BF16 = mybir.dt.bfloat16
+U32 = mybir.dt.uint32
+U16 = mybir.dt.uint16
+U8 = mybir.dt.uint8
+E4M3 = mybir.dt.float8_e4m3fn_x4
+E5M2 = mybir.dt.float8_e5m2_x4
+ALU = mybir.AluOpType
+ACT = mybir.ActivationFunctionType
+
+P = 128
+PACK = 4
+K_PASS = P * PACK
+ROW_PASSES = R // K_PASS
+BLOCKS = D // P
+RUN = 4
+
+
+def tile_attend_ghub_ada_kernel(tc, xT, wT, y, wt, xm, vT, offs, out_0, out_1):
+    nc = tc.nc
+    with ExitStack() as ctx:
+        keep = ctx.enter_context(tc.tile_pool(name="keep", bufs=1))
+        tables = ctx.enter_context(tc.tile_pool(name="tables", bufs=4))
+        work = ctx.enter_context(tc.tile_pool(name="work", bufs=2))
+        psum = ctx.enter_context(tc.psum_pool(name="psum", bufs=4))
+
+        def quantize(name, grouped, fmt):
+            width = grouped.shape[1] // PACK
+            codes = keep.tile([P, width], U32, name=name + "_codes", align_bytes=64)
+            scales = keep.tile([P, width], U8, name=name + "_scales", align_bytes=64)
+            nc.vector.quantize_mx(out=codes[:].bitcast(fmt), scales=scales[:], in_=grouped)
+            return codes, scales
+
+        big = keep.tile([P, 1], F32, name="big")
+        guard = keep.tile([P, 1], F32, name="guard")
+        one = keep.tile([P, 1], F32, name="one")
+        eps = keep.tile([P, 1], F32, name="eps")
+        nc.vector.memset(big[:], 2.0 ** 80)
+        nc.scalar.activation(out=big[:], in_=big[:], func=ACT.Abs_reciprocal_sqrt)
+        nc.scalar.activation(out=guard[:], in_=big[:], func=ACT.Square)
+        nc.vector.memset(one[:], 1.0)
+        nc.vector.tensor_scalar(out=eps[:], in0=one[:], scalar1=EPS, scalar2=None, op0=ALU.mult)
+
+        steps = [keep.tile([P, T], F32, name="step%d" % j) for j in range(BLOCKS)]
+        for j in range(BLOCKS):
+            nc.vector.memset(steps[j][:], 0.0)
+
+        offsets = keep.tile([P, N // 16], U16, name="offsets")
+        w_planes = [tables.tile([P, T], F32, name="w%d" % j, tag="table") for j in range(PACK)]
+        w_rows = wT.rearrange("(p j) c -> p j c", j=PACK)
+        nc.sync.dma_start(out=w_planes[0][:], in_=w_rows[:, 0, :])
+        nc.sync.dma_start(offsets[:], offs)
+        for j in range(1, PACK):
+            nc.sync.dma_start(out=w_planes[j][:], in_=w_rows[:, j, :])
+        weight = keep.tile([P, ROW_PASSES, PACK], F32, name="weight")
+        x_raw = [keep.tile([P, PACK, K_PASS], F32, name="x_raw%d" % g) for g in range(ROW_PASSES)]
+        y_t = [keep.tile([P, PACK, N], F32, name="y%d" % g) for g in range(ROW_PASSES)]
+        x_rows = xT[0].rearrange("(p j) r -> p j r", j=PACK)
+        y_rows = y[0].rearrange("(g p t) i -> g p t i", g=ROW_PASSES, t=PACK)
+        nc.sync.dma_start(out=weight[:], in_=wt[0].rearrange("(g p t) o -> p g (t o)", g=ROW_PASSES, t=PACK))
+        for g in range(ROW_PASSES):
+            nc.sync.dma_start(out=x_raw[g][:], in_=x_rows[:, :, g * K_PASS:(g + 1) * K_PASS])
+            for h in range(2):
+                nc.sync.dma_start(out=y_t[g][:, 2 * h:2 * h + 2, :], in_=y_rows[g, :, 2 * h:2 * h + 2, :])
+        xm_raw = [keep.tile([P, PACK, D], F32, name="xm_raw%d" % g) for g in range(ROW_PASSES)]
+        xm_rows = xm[0].rearrange("(g p t) d -> g p t d", g=ROW_PASSES, t=PACK)
+        v_planes = [keep.tile([P, T], F32, name="v%d" % j) for j in range(BLOCKS)]
+        for g in range(ROW_PASSES):
+            nc.sync.dma_start(out=xm_raw[g][:, :, 0:P], in_=xm_rows[g, :, :, 0:P])
+        nc.sync.dma_start(out=v_planes[0][:], in_=vT[0:P, :])
+        for g in range(ROW_PASSES):
+            nc.sync.dma_start(out=xm_raw[g][:, :, P:D], in_=xm_rows[g, :, :, P:D])
+        for j in range(1, BLOCKS):
+            nc.sync.dma_start(out=v_planes[j][:], in_=vT[j * P:(j + 1) * P, :])
+
+        w_grouped = keep.tile([P, N, PACK], BF16, name="w_grouped", align_bytes=64)
+        for j in range(PACK):
+            nc.vector.tensor_copy(out=w_grouped[:, :, j], in_=w_planes[j][:].indirect(offsets[:]))
+        w_codes, w_scales = quantize("w", w_grouped[:].rearrange("p n j -> p (n j)"), E4M3)
+
+        neg_weight = keep.tile([P, ROW_PASSES, PACK], F32, name="neg_weight")
+        upper = keep.tile([P, ROW_PASSES, PACK], F32, name="upper")
+        lower = keep.tile([P, ROW_PASSES, PACK], F32, name="lower")
+        nc.vector.tensor_scalar(out=neg_weight[:], in0=weight[:], scalar1=-1.0, scalar2=None, op0=ALU.mult)
+        nc.vector.tensor_tensor(out=upper[:], in0=weight[:], in1=neg_weight[:], op=ALU.max)
+        nc.vector.tensor_tensor(out=lower[:], in0=weight[:], in1=neg_weight[:], op=ALU.min)
+
+        g_quant = []
+        for g in range(ROW_PASSES):
+            x_grouped = work.tile([P, K_PASS, PACK], BF16, name="x_grouped", align_bytes=64)
+            dst = x_grouped[:].rearrange("p (t m) j -> p m t j", t=PACK)
+            src = x_raw[g][:].rearrange("p j (m t) -> p m t j", t=PACK)
+            if g == 0:
+                nc.vector.tensor_copy(out=dst, in_=src)
+            else:
+                nc.scalar.copy(out=dst, in_=src)
+            x_codes, x_scales = quantize("x%d" % g, x_grouped[:].rearrange("p c j -> p (c j)"), E4M3)
+            clipped = work.tile([P, PACK, N], BF16, name="clipped", align_bytes=64)
+            for t in range(PACK):
+                w_col = weight[:, g, t:t + 1]
+                nc.scalar.activation(out=y_t[g][:, t, :], in_=y_t[g][:, t, :], func=ACT.Copy, scale=w_col)
+                acc = psum.tile([P, N], F32, name="acc")
+                cols = slice(t * P, (t + 1) * P)
+                nc.tensor.matmul_mx(out=acc[:], lhsT=x_codes[:, cols].bitcast(E4M3), lhsT_scale=x_scales[:, cols],
+                                    rhs=w_codes[:].bitcast(E4M3), rhs_scale=w_scales[:], start=True, stop=True)
+                nc.vector.scalar_tensor_tensor(out=y_t[g][:, t, :], in0=acc[:], scalar=w_col, in1=y_t[g][:, t, :],
+                                               op0=ALU.mult, op1=ALU.subtract)
+            for t in range(PACK):
+                nc.vector.tensor_scalar(out=clipped[:, t, :], in0=y_t[g][:, t, :], scalar1=lower[:, g, t:t + 1],
+                                        scalar2=upper[:, g, t:t + 1], op0=ALU.max, op1=ALU.min)
+            g_grouped = work.tile([P, N, PACK], BF16, name="g_grouped", align_bytes=64)
+            nc.vector.tensor_copy(out=g_grouped[:].rearrange("p (c i) t -> p c t i", i=RUN),
+                                  in_=clipped[:].rearrange("p t (c i) -> p c t i", i=RUN))
+            g_quant.append(quantize("g%d" % g, g_grouped[:].rearrange("p n t -> p (n t)"), E5M2))
+
+        def prepare(j):
+            d_cols = slice(j * P, (j + 1) * P)
+            xm_grouped = work.tile([P, ROW_PASSES, P, PACK], BF16, name="xm_grouped", align_bytes=64)
+            for g in range(ROW_PASSES):
+                nc.scalar.copy(out=xm_grouped[:, g].rearrange("p (c i) t -> p c t i", i=RUN),
+                               in_=xm_raw[g][:, :, d_cols].rearrange("p t (c i) -> p c t i", i=RUN))
+            xm_codes, xm_scales = quantize("xm%d" % j, xm_grouped[:].rearrange("p g d t -> p (g d t)"), E4M3)
+            dw = psum.tile([P, N], F32, name="dw")
+            for g in range(ROW_PASSES):
+                cols = slice(g * P, (g + 1) * P)
+                nc.tensor.matmul_mx(out=dw[:], lhsT=xm_codes[:, cols].bitcast(E4M3), lhsT_scale=xm_scales[:, cols],
+                                    rhs=g_quant[g][0][:].bitcast(E5M2), rhs_scale=g_quant[g][1][:],
+                                    start=(g == 0), stop=(g == ROW_PASSES - 1))
+            picked = work.tile([P, N], F32, name="picked")
+            nc.vector.tensor_copy(out=picked[:], in_=v_planes[j][:].indirect(offsets[:]))
+            square = work.tile([P, N], F32, name="square")
+            nc.scalar.activation(out=square[:], in_=dw[:], func=ACT.Square)
+            nv = work.tile([P, N], F32, name="nv")
+            nc.vector.tensor_tensor(out=nv[:], in0=picked[:], in1=square[:], op=ALU.add)
+            descent = work.tile([P, N], F32, name="descent")
+            nc.scalar.activation(out=descent[:], in_=dw[:], func=ACT.Copy, scale=-LR)
+            inv = work.tile([P, N], F32, name="inv")
+            nc.scalar.activation(out=inv[:], in_=nv[:], func=ACT.Abs_reciprocal_sqrt, bias=guard[:])
+            nc.scalar.activation(out=inv[:], in_=inv[:], func=ACT.Square)
+            nc.scalar.activation(out=inv[:], in_=inv[:], func=ACT.Abs_reciprocal_sqrt)
+            nc.scalar.activation(out=inv[:], in_=inv[:], func=ACT.Square, bias=eps[:])
+            nc.scalar.activation(out=inv[:], in_=inv[:], func=ACT.Abs_reciprocal_sqrt)
+            v_new = tables.tile([P, T], F32, name="v_new%d" % j, tag="table")
+            for h in range(2):
+                half = slice(h * T // 2, (h + 1) * T // 2)
+                nc.scalar.activation(out=v_new[:, half], in_=v_planes[j][:, half], func=ACT.Copy)
+            return nv, descent, inv, v_new
+
+        ready = prepare(0)
+        for j in range(BLOCKS):
+            nv, descent, inv, v_new = ready
+            rows = slice(j * P, (j + 1) * P)
+            nc.vector.tensor_copy(out=v_new[:].indirect(offsets[:]), in_=nv[:])
+            nc.sync.dma_start(out=out_1[rows, :], in_=v_new[:])
+            if j + 1 < BLOCKS:
+                ready = prepare(j + 1)
+            nc.vector.tensor_tensor(out=steps[j][:].indirect(offsets[:]), in0=descent[:], in1=inv[:], op=ALU.mult)
+            nc.sync.dma_start(out=out_0[rows, :], in_=steps[j][:])

@@ -23,6 +23,9 @@ K_PASS = P * PACK
 ROW_PASSES = R // K_PASS
 BLOCKS = D // P
 RUN = 4
+X_PIECES = (((0, 256), (256, 512)), ((0, 512),))
+X_CASTS = (((0, 64, True), (64, 128, True)), ((0, 64, False), (64, 128, True)))
+IL_SPLIT = (0, 64)
 
 
 def tile_attend_ghub_ada_kernel(tc, xT, wT, y, wt, xm, vT, offs, out_0, out_1):
@@ -31,6 +34,7 @@ def tile_attend_ghub_ada_kernel(tc, xT, wT, y, wt, xm, vT, offs, out_0, out_1):
         keep = ctx.enter_context(tc.tile_pool(name="keep", bufs=1))
         tables = ctx.enter_context(tc.tile_pool(name="tables", bufs=4))
         work = ctx.enter_context(tc.tile_pool(name="work", bufs=2))
+        tail = ctx.enter_context(tc.tile_pool(name="tail", bufs=4))
         psum = ctx.enter_context(tc.psum_pool(name="psum", bufs=4))
 
         def quantize(name, grouped, fmt):
@@ -50,8 +54,8 @@ def tile_attend_ghub_ada_kernel(tc, xT, wT, y, wt, xm, vT, offs, out_0, out_1):
         nc.vector.memset(one[:], 1.0)
         nc.vector.tensor_scalar(out=eps[:], in0=one[:], scalar1=EPS, scalar2=None, op0=ALU.mult)
 
-        steps = [keep.tile([P, T], F32, name="step%d" % j) for j in range(BLOCKS)]
-        for j in range(BLOCKS):
+        steps = [keep.tile([P, T], F32, name="step%d" % j) for j in range(2)]
+        for j in range(2):
             nc.vector.memset(steps[j][:], 0.0)
 
         offsets = keep.tile([P, N // 16], U16, name="offsets")
@@ -68,18 +72,23 @@ def tile_attend_ghub_ada_kernel(tc, xT, wT, y, wt, xm, vT, offs, out_0, out_1):
         y_rows = y[0].rearrange("(g p t) i -> g p t i", g=ROW_PASSES, t=PACK)
         nc.sync.dma_start(out=weight[:], in_=wt[0].rearrange("(g p t) o -> p g (t o)", g=ROW_PASSES, t=PACK))
         for g in range(ROW_PASSES):
-            nc.sync.dma_start(out=x_raw[g][:], in_=x_rows[:, :, g * K_PASS:(g + 1) * K_PASS])
+            for lo, hi in X_PIECES[g]:
+                nc.sync.dma_start(out=x_raw[g][:, :, lo:hi], in_=x_rows[:, :, g * K_PASS + lo:g * K_PASS + hi])
             for h in range(2):
                 nc.sync.dma_start(out=y_t[g][:, 2 * h:2 * h + 2, :], in_=y_rows[g, :, 2 * h:2 * h + 2, :])
-        xm_raw = [keep.tile([P, PACK, D], F32, name="xm_raw%d" % g) for g in range(ROW_PASSES)]
+        xm_first = keep.tile([P, ROW_PASSES, PACK, P], F32, name="xm_first", tag="slot_a", align_bytes=64)
+        xm_rest = [keep.tile([P, PACK, D - P], F32, name="xm_rest%d" % g) for g in range(ROW_PASSES)]
         xm_rows = xm[0].rearrange("(g p t) d -> g p t d", g=ROW_PASSES, t=PACK)
-        v_planes = [keep.tile([P, T], F32, name="v%d" % j) for j in range(BLOCKS)]
+        v_planes = [keep.tile([P, T], F32, name="v%d" % j, tag="slot_v%d" % j, align_bytes=64) for j in range(BLOCKS)]
         for g in range(ROW_PASSES):
-            nc.sync.dma_start(out=xm_raw[g][:, :, 0:P], in_=xm_rows[g, :, :, 0:P])
+            nc.sync.dma_start(out=xm_first[:, g], in_=xm_rows[g, :, :, 0:P])
+        v_loaded = keep.tile([P, T], F32, name="v_loaded")
         nc.sync.dma_start(out=v_planes[0][:], in_=vT[0:P, :])
+        nc.sync.dma_start(out=v_planes[1][:], in_=vT[P:2 * P, :])
+        nc.sync.dma_start(out=v_loaded[:], in_=vT[0:P, :])
         for g in range(ROW_PASSES):
-            nc.sync.dma_start(out=xm_raw[g][:, :, P:D], in_=xm_rows[g, :, :, P:D])
-        for j in range(1, BLOCKS):
+            nc.sync.dma_start(out=xm_rest[g][:], in_=xm_rows[g, :, :, P:D])
+        for j in range(2, BLOCKS):
             nc.sync.dma_start(out=v_planes[j][:], in_=vT[j * P:(j + 1) * P, :])
 
         w_grouped = keep.tile([P, N, PACK], BF16, name="w_grouped", align_bytes=64)
@@ -94,74 +103,121 @@ def tile_attend_ghub_ada_kernel(tc, xT, wT, y, wt, xm, vT, offs, out_0, out_1):
         nc.vector.tensor_tensor(out=upper[:], in0=weight[:], in1=neg_weight[:], op=ALU.max)
         nc.vector.tensor_tensor(out=lower[:], in0=weight[:], in1=neg_weight[:], op=ALU.min)
 
-        g_quant = []
-        for g in range(ROW_PASSES):
+        def first_product(g):
             x_grouped = work.tile([P, K_PASS, PACK], BF16, name="x_grouped", align_bytes=64)
             dst = x_grouped[:].rearrange("p (t m) j -> p m t j", t=PACK)
             src = x_raw[g][:].rearrange("p j (m t) -> p m t j", t=PACK)
-            if g == 0:
-                nc.vector.tensor_copy(out=dst, in_=src)
-            else:
-                nc.scalar.copy(out=dst, in_=src)
-            x_codes, x_scales = quantize("x%d" % g, x_grouped[:].rearrange("p c j -> p (c j)"), E4M3)
-            clipped = work.tile([P, PACK, N], BF16, name="clipped", align_bytes=64)
+            for lo, hi, on_vector in X_CASTS[g]:
+                if on_vector:
+                    nc.vector.tensor_copy(out=dst[:, lo:hi], in_=src[:, lo:hi])
+                else:
+                    nc.scalar.copy(out=dst[:, lo:hi], in_=src[:, lo:hi])
+            x_codes = keep.tile([P, K_PASS], U32, name="x_codes%d" % g, align_bytes=64)
+            x_scales = keep.tile([P, K_PASS], U8, name="x_scales%d" % g, align_bytes=64)
+            parts = 4 if g == 0 else 1
+            for c in range(parts):
+                cols = slice(c * K_PASS // parts, (c + 1) * K_PASS // parts)
+                nc.vector.quantize_mx(out=x_codes[:, cols].bitcast(E4M3), scales=x_scales[:, cols],
+                                      in_=x_grouped[:, cols, :].rearrange("p c j -> p (c j)"))
+            banks = []
             for t in range(PACK):
-                w_col = weight[:, g, t:t + 1]
-                nc.scalar.activation(out=y_t[g][:, t, :], in_=y_t[g][:, t, :], func=ACT.Copy, scale=w_col)
+                nc.scalar.activation(out=y_t[g][:, t, :], in_=y_t[g][:, t, :], func=ACT.Copy,
+                                     scale=weight[:, g, t:t + 1])
                 acc = psum.tile([P, N], F32, name="acc")
                 cols = slice(t * P, (t + 1) * P)
                 nc.tensor.matmul_mx(out=acc[:], lhsT=x_codes[:, cols].bitcast(E4M3), lhsT_scale=x_scales[:, cols],
                                     rhs=w_codes[:].bitcast(E4M3), rhs_scale=w_scales[:], start=True, stop=True)
-                nc.vector.scalar_tensor_tensor(out=y_t[g][:, t, :], in0=acc[:], scalar=w_col, in1=y_t[g][:, t, :],
-                                               op0=ALU.mult, op1=ALU.subtract)
+                banks.append(acc)
+            return banks
+
+        def clip(g, banks):
+            clipped = work.tile([P, PACK, N], BF16, name="clipped", align_bytes=64)
+            for t in range(PACK):
+                nc.vector.scalar_tensor_tensor(out=y_t[g][:, t, :], in0=banks[t][:], scalar=weight[:, g, t:t + 1],
+                                               in1=y_t[g][:, t, :], op0=ALU.mult, op1=ALU.subtract)
             for t in range(PACK):
                 nc.vector.tensor_scalar(out=clipped[:, t, :], in0=y_t[g][:, t, :], scalar1=lower[:, g, t:t + 1],
                                         scalar2=upper[:, g, t:t + 1], op0=ALU.max, op1=ALU.min)
-            g_grouped = work.tile([P, N, PACK], BF16, name="g_grouped", align_bytes=64)
-            nc.vector.tensor_copy(out=g_grouped[:].rearrange("p (c i) t -> p c t i", i=RUN),
-                                  in_=clipped[:].rearrange("p t (c i) -> p c t i", i=RUN))
-            g_quant.append(quantize("g%d" % g, g_grouped[:].rearrange("p n t -> p (n t)"), E5M2))
+            return clipped
 
-        def prepare(j):
-            d_cols = slice(j * P, (j + 1) * P)
-            xm_grouped = work.tile([P, ROW_PASSES, P, PACK], BF16, name="xm_grouped", align_bytes=64)
+        def quantize_g(g, clipped):
+            g_grouped = keep.tile([P, N, PACK], BF16, name="g_grouped%d" % g, tag="slot_a" if g == 0 else "slot_g", align_bytes=64)
+            dst = g_grouped[:].rearrange("p (c i) t -> p c t i", i=RUN)
+            src = clipped[:].rearrange("p t (c i) -> p c t i", i=RUN)
+            split = IL_SPLIT[g]
+            if split < N // RUN:
+                nc.scalar.copy(out=dst[:, split:], in_=src[:, split:])
+            if split > 0:
+                nc.vector.tensor_copy(out=dst[:, :split], in_=src[:, :split])
+            scales = keep.tile([P, N], U8, name="g_scales%d" % g, align_bytes=64)
+            nc.vector.quantize_mx(out=g_codes[:, g].bitcast(E5M2), scales=scales[:],
+                                  in_=g_grouped[:].rearrange("p n t -> p (n t)"))
+            return g_codes[:, g], scales
+
+        def quantize_xm(j):
+            xm_grouped = tail.tile([P, ROW_PASSES, P, PACK], BF16, name="xm_grouped", align_bytes=64)
             for g in range(ROW_PASSES):
+                raw = xm_first[:, g] if j == 0 else xm_rest[g][:, :, (j - 1) * P:j * P]
                 nc.scalar.copy(out=xm_grouped[:, g].rearrange("p (c i) t -> p c t i", i=RUN),
-                               in_=xm_raw[g][:, :, d_cols].rearrange("p t (c i) -> p c t i", i=RUN))
-            xm_codes, xm_scales = quantize("xm%d" % j, xm_grouped[:].rearrange("p g d t -> p (g d t)"), E4M3)
-            dw = psum.tile([P, N], F32, name="dw")
-            for g in range(ROW_PASSES):
-                cols = slice(g * P, (g + 1) * P)
-                nc.tensor.matmul_mx(out=dw[:], lhsT=xm_codes[:, cols].bitcast(E4M3), lhsT_scale=xm_scales[:, cols],
-                                    rhs=g_quant[g][0][:].bitcast(E5M2), rhs_scale=g_quant[g][1][:],
-                                    start=(g == 0), stop=(g == ROW_PASSES - 1))
-            picked = work.tile([P, N], F32, name="picked")
-            nc.vector.tensor_copy(out=picked[:], in_=v_planes[j][:].indirect(offsets[:]))
-            square = work.tile([P, N], F32, name="square")
-            nc.scalar.activation(out=square[:], in_=dw[:], func=ACT.Square)
-            nv = work.tile([P, N], F32, name="nv")
-            nc.vector.tensor_tensor(out=nv[:], in0=picked[:], in1=square[:], op=ALU.add)
-            descent = work.tile([P, N], F32, name="descent")
-            nc.scalar.activation(out=descent[:], in_=dw[:], func=ACT.Copy, scale=-LR)
-            inv = work.tile([P, N], F32, name="inv")
-            nc.scalar.activation(out=inv[:], in_=nv[:], func=ACT.Abs_reciprocal_sqrt, bias=guard[:])
-            nc.scalar.activation(out=inv[:], in_=inv[:], func=ACT.Square)
-            nc.scalar.activation(out=inv[:], in_=inv[:], func=ACT.Abs_reciprocal_sqrt)
-            nc.scalar.activation(out=inv[:], in_=inv[:], func=ACT.Square, bias=eps[:])
-            nc.scalar.activation(out=inv[:], in_=inv[:], func=ACT.Abs_reciprocal_sqrt)
+                               in_=raw.rearrange("p t (c i) -> p c t i", i=RUN))
+            return quantize("xm%d" % j, xm_grouped[:].rearrange("p g d t -> p (g d t)"), E4M3)
+
+        def gather_v(j):
+            nv = tail.tile([P, N], F32, name="nv")
+            nc.vector.tensor_copy(out=nv[:], in_=v_planes[j][:].indirect(offsets[:]))
+            return nv
+
+        def copy_v(j):
             v_new = tables.tile([P, T], F32, name="v_new%d" % j, tag="table")
             for h in range(2):
                 half = slice(h * T // 2, (h + 1) * T // 2)
                 nc.scalar.activation(out=v_new[:, half], in_=v_planes[j][:, half], func=ACT.Copy)
-            return nv, descent, inv, v_new
+            return v_new
 
-        ready = prepare(0)
+        clipped0 = clip(0, first_product(0))
+        banks1 = first_product(1)
+        clipped1 = clip(1, banks1)
+        xm_quant = [quantize_xm(0)]
+        picked = [gather_v(0)]
+        g_codes = keep.tile([P, ROW_PASSES, N], U32, name="g_codes", tag="slot_v0", align_bytes=64)
+        g_quant = [quantize_g(0, clipped0)]
+        g_quant.append(quantize_g(1, clipped1))
+        picked.append(gather_v(1))
+        windows = [v_loaded, copy_v(1)]
+
+        def second_product(j):
+            if j > 0:
+                xm_quant.append(quantize_xm(j))
+            xm_codes, xm_scales = xm_quant[j]
+            dw = psum.tile([P, N], F32, name="dw")
+            for g in range(ROW_PASSES):
+                cols = slice(g * P, (g + 1) * P)
+                nc.tensor.matmul_mx(out=dw[:], lhsT=xm_codes[:, cols].bitcast(E4M3), lhsT_scale=xm_scales[:, cols],
+                                    rhs=g_quant[g][0].bitcast(E5M2), rhs_scale=g_quant[g][1][:],
+                                    start=(g == 0), stop=(g == ROW_PASSES - 1))
+            if j > 1:
+                picked.append(gather_v(j))
+            nv = keep.tile([P, N], F32, name="nv0", tag="slot_v1", align_bytes=64) if j == 0 else picked[j]
+            inv = tail.tile([P, N], F32, name="inv")
+            nc.scalar.activation(out=inv[:], in_=dw[:], func=ACT.Square)
+            nc.vector.tensor_tensor(out=nv[:], in0=picked[j][:], in1=inv[:], op=ALU.add)
+            return dw, nv, inv
+
+        products = [second_product(j) for j in range(BLOCKS)]
         for j in range(BLOCKS):
-            nv, descent, inv, v_new = ready
+            dw, nv, inv = products[j]
             rows = slice(j * P, (j + 1) * P)
+            if j > 1:
+                windows.append(copy_v(j))
+            v_new = windows[j]
             nc.vector.tensor_copy(out=v_new[:].indirect(offsets[:]), in_=nv[:])
             nc.sync.dma_start(out=out_1[rows, :], in_=v_new[:])
-            if j + 1 < BLOCKS:
-                ready = prepare(j + 1)
-            nc.vector.tensor_tensor(out=steps[j][:].indirect(offsets[:]), in0=descent[:], in1=inv[:], op=ALU.mult)
-            nc.sync.dma_start(out=out_0[rows, :], in_=steps[j][:])
+            descent = tail.tile([P, N], F32, name="descent")
+            nc.scalar.activation(out=inv[:], in_=nv[:], func=ACT.Abs_reciprocal_sqrt, bias=guard[:])
+            nc.scalar.activation(out=descent[:], in_=dw[:], func=ACT.Copy, scale=-LR)
+            nc.scalar.activation(out=inv[:], in_=inv[:], func=ACT.Square)
+            nc.scalar.activation(out=inv[:], in_=inv[:], func=ACT.Abs_reciprocal_sqrt)
+            nc.scalar.activation(out=inv[:], in_=inv[:], func=ACT.Square, bias=eps[:])
+            nc.scalar.activation(out=inv[:], in_=inv[:], func=ACT.Abs_reciprocal_sqrt)
+            nc.vector.tensor_tensor(out=steps[j % 2][:].indirect(offsets[:]), in0=descent[:], in1=inv[:], op=ALU.mult)
+            nc.sync.dma_start(out=out_0[rows, :], in_=steps[j % 2][:])

@@ -23,9 +23,10 @@ K_PASS = P * PACK
 ROW_PASSES = R // K_PASS
 BLOCKS = D // P
 RUN = 4
+Y_PIECES = (((0, 1), (1, 2), (2, 4)), ((0, 2), (2, 4)))
 X_PIECES = (((0, 256), (256, 512)), ((0, 512),))
-X_CASTS = (((0, 64, True), (64, 128, True)), ((0, 64, False), (64, 128, True)))
-IL_SPLIT = (0, 64)
+X_CASTS = (((0, 64, False), (64, 128, True)), ((0, 64, False), (64, 128, True)))
+IL_SPLIT = (0, 32)
 
 
 def tile_attend_ghub_ada_kernel(tc, xT, wT, y, wt, xm, vT, offs, out_0, out_1):
@@ -74,8 +75,8 @@ def tile_attend_ghub_ada_kernel(tc, xT, wT, y, wt, xm, vT, offs, out_0, out_1):
         for g in range(ROW_PASSES):
             for lo, hi in X_PIECES[g]:
                 nc.sync.dma_start(out=x_raw[g][:, :, lo:hi], in_=x_rows[:, :, g * K_PASS + lo:g * K_PASS + hi])
-            for h in range(2):
-                nc.sync.dma_start(out=y_t[g][:, 2 * h:2 * h + 2, :], in_=y_rows[g, :, 2 * h:2 * h + 2, :])
+            for lo, hi in Y_PIECES[g]:
+                nc.sync.dma_start(out=y_t[g][:, lo:hi, :], in_=y_rows[g, :, lo:hi, :])
         xm_first = keep.tile([P, ROW_PASSES, PACK, P], F32, name="xm_first", tag="slot_a", align_bytes=64)
         xm_rest = [keep.tile([P, PACK, D - P], F32, name="xm_rest%d" % g) for g in range(ROW_PASSES)]
         xm_rows = xm[0].rearrange("(g p t) d -> g p t d", g=ROW_PASSES, t=PACK)
@@ -200,7 +201,8 @@ def tile_attend_ghub_ada_kernel(tc, xT, wT, y, wt, xm, vT, offs, out_0, out_1):
             nv = keep.tile([P, N], F32, name="nv0", tag="slot_v1", align_bytes=64) if j == 0 else picked[j]
             inv = tail.tile([P, N], F32, name="inv")
             nc.scalar.activation(out=inv[:], in_=dw[:], func=ACT.Square)
-            nc.vector.tensor_tensor(out=nv[:], in0=picked[j][:], in1=inv[:], op=ALU.add)
+            adder = nc.vector if j == 0 else nc.gpsimd
+            adder.tensor_tensor(out=nv[:], in0=picked[j][:], in1=inv[:], op=ALU.add)
             return dw, nv, inv
 
         products = [second_product(j) for j in range(BLOCKS)]

@@ -78,17 +78,20 @@ def tile_attend_ghub_ada_kernel(tc, xT, wT, y, wt, xm, vT, offs, out_0, out_1):
             for lo, hi in Y_PIECES[g]:
                 nc.sync.dma_start(out=y_t[g][:, lo:hi, :], in_=y_rows[g, :, lo:hi, :])
         xm_first = keep.tile([P, ROW_PASSES, PACK, P], F32, name="xm_first", tag="slot_a", align_bytes=64)
-        xm_rest = [keep.tile([P, PACK, D - P], F32, name="xm_rest%d" % g) for g in range(ROW_PASSES)]
+        xm_second = keep.tile([P, ROW_PASSES, PACK, P], F32, name="xm_second")
+        xm_rest = [keep.tile([P, PACK, D - 2 * P], F32, name="xm_rest%d" % g) for g in range(ROW_PASSES)]
         xm_rows = xm[0].rearrange("(g p t) d -> g p t d", g=ROW_PASSES, t=PACK)
         v_planes = [keep.tile([P, T], F32, name="v%d" % j, tag="slot_v%d" % j, align_bytes=64) for j in range(BLOCKS)]
         for g in range(ROW_PASSES):
             nc.sync.dma_start(out=xm_first[:, g], in_=xm_rows[g, :, :, 0:P])
+        for g in range(ROW_PASSES):
+            nc.sync.dma_start(out=xm_second[:, g], in_=xm_rows[g, :, :, P:2 * P])
         v_loaded = keep.tile([P, T], F32, name="v_loaded")
         nc.sync.dma_start(out=v_planes[0][:], in_=vT[0:P, :])
-        nc.sync.dma_start(out=v_planes[1][:], in_=vT[P:2 * P, :])
         nc.sync.dma_start(out=v_loaded[:], in_=vT[0:P, :])
+        nc.sync.dma_start(out=v_planes[1][:], in_=vT[P:2 * P, :])
         for g in range(ROW_PASSES):
-            nc.sync.dma_start(out=xm_rest[g][:], in_=xm_rows[g, :, :, P:D])
+            nc.sync.dma_start(out=xm_rest[g][:], in_=xm_rows[g, :, :, 2 * P:D])
         for j in range(2, BLOCKS):
             nc.sync.dma_start(out=v_planes[j][:], in_=vT[j * P:(j + 1) * P, :])
 
@@ -158,13 +161,13 @@ def tile_attend_ghub_ada_kernel(tc, xT, wT, y, wt, xm, vT, offs, out_0, out_1):
         def quantize_xm(j):
             xm_grouped = tail.tile([P, ROW_PASSES, P, PACK], BF16, name="xm_grouped", align_bytes=64)
             for g in range(ROW_PASSES):
-                raw = xm_first[:, g] if j == 0 else xm_rest[g][:, :, (j - 1) * P:j * P]
+                raw = (xm_first, xm_second)[j][:, g] if j < 2 else xm_rest[g][:, :, (j - 2) * P:(j - 1) * P]
                 nc.scalar.copy(out=xm_grouped[:, g].rearrange("p (c i) t -> p c t i", i=RUN),
                                in_=raw.rearrange("p t (c i) -> p c t i", i=RUN))
             return quantize("xm%d" % j, xm_grouped[:].rearrange("p g d t -> p (g d t)"), E4M3)
 
         def gather_v(j):
-            nv = tail.tile([P, N], F32, name="nv")
+            nv = keep.tile([P, N], F32, name="nv%d" % j, tag="slot_g" if j == 0 else "nv%d" % j, align_bytes=64)
             nc.vector.tensor_copy(out=nv[:], in_=v_planes[j][:].indirect(offsets[:]))
             return nv
 
@@ -179,12 +182,11 @@ def tile_attend_ghub_ada_kernel(tc, xT, wT, y, wt, xm, vT, offs, out_0, out_1):
         banks1 = first_product(1)
         clipped1 = clip(1, banks1)
         xm_quant = [quantize_xm(0)]
-        picked = [gather_v(0)]
-        g_codes = keep.tile([P, ROW_PASSES, N], U32, name="g_codes", tag="slot_v0", align_bytes=64)
+        g_codes = keep.tile([P, ROW_PASSES, N], U32, name="g_codes", align_bytes=64)
         g_quant = [quantize_g(0, clipped0)]
         g_quant.append(quantize_g(1, clipped1))
-        picked.append(gather_v(1))
-        windows = [v_loaded, copy_v(1)]
+        picked = [gather_v(0)]
+        windows = [v_loaded]
 
         def second_product(j):
             if j > 0:
@@ -196,9 +198,9 @@ def tile_attend_ghub_ada_kernel(tc, xT, wT, y, wt, xm, vT, offs, out_0, out_1):
                 nc.tensor.matmul_mx(out=dw[:], lhsT=xm_codes[:, cols].bitcast(E4M3), lhsT_scale=xm_scales[:, cols],
                                     rhs=g_quant[g][0].bitcast(E5M2), rhs_scale=g_quant[g][1][:],
                                     start=(g == 0), stop=(g == ROW_PASSES - 1))
-            if j > 1:
+            if j > 0:
                 picked.append(gather_v(j))
-            nv = keep.tile([P, N], F32, name="nv0", tag="slot_v1", align_bytes=64) if j == 0 else picked[j]
+            nv = picked[j]
             inv = tail.tile([P, N], F32, name="inv")
             nc.scalar.activation(out=inv[:], in_=dw[:], func=ACT.Square)
             adder = nc.vector if j == 0 else nc.gpsimd
@@ -209,7 +211,7 @@ def tile_attend_ghub_ada_kernel(tc, xT, wT, y, wt, xm, vT, offs, out_0, out_1):
         for j in range(BLOCKS):
             dw, nv, inv = products[j]
             rows = slice(j * P, (j + 1) * P)
-            if j > 1:
+            if j > 0:
                 windows.append(copy_v(j))
             v_new = windows[j]
             nc.vector.tensor_copy(out=v_new[:].indirect(offsets[:]), in_=nv[:])

@@ -24,109 +24,116 @@ ROW_PASSES = R // K_PASS
 BLOCKS = D // P
 RUN = 4
 Y_PIECES = (((0, 1), (1, 2), (2, 4)), ((0, 2), (2, 4)))
-X_PIECES = (((0, 256), (256, 512)), ((0, 512),))
-X_CASTS = (((0, 64, False), (64, 128, True)), ((0, 64, False), (64, 128, True)))
-IL_SPLIT = (0, 32)
+X_PIECES = ((0, 256), (256, 512))
+IL_SPLIT = (0, 0)
+REGION = 10
+Y1_AT = REGION * PACK
 
 
 def tile_attend_ghub_ada_kernel(tc, xT, wT, y, wt, xm, vT, offs, out_0, out_1):
     nc = tc.nc
     with ExitStack() as ctx:
         keep = ctx.enter_context(tc.tile_pool(name="keep", bufs=1))
-        tables = ctx.enter_context(tc.tile_pool(name="tables", bufs=4))
-        work = ctx.enter_context(tc.tile_pool(name="work", bufs=2))
-        tail = ctx.enter_context(tc.tile_pool(name="tail", bufs=4))
+        handed = ctx.enter_context(tc.tile_pool(name="handed", bufs=1))
         psum = ctx.enter_context(tc.psum_pool(name="psum", bufs=4))
 
-        def quantize(name, grouped, fmt):
-            width = grouped.shape[1] // PACK
-            codes = keep.tile([P, width], U32, name=name + "_codes", align_bytes=64)
-            scales = keep.tile([P, width], U8, name=name + "_scales", align_bytes=64)
-            nc.vector.quantize_mx(out=codes[:].bitcast(fmt), scales=scales[:], in_=grouped)
-            return codes, scales
+        def held(shape, dtype, name, slot=None):
+            return keep.tile(shape, dtype, name=name, tag=slot or name, align_bytes=64)
 
-        big = keep.tile([P, 1], F32, name="big")
-        guard = keep.tile([P, 1], F32, name="guard")
-        one = keep.tile([P, 1], F32, name="one")
-        eps = keep.tile([P, 1], F32, name="eps")
+        def placed(shape, dtype, name, kib):
+            return handed.tile(shape, dtype, name=name, offset=kib * 1024, align_bytes=64)
+
+        big = held([P, 1], F32, "big")
+        guard = held([P, 1], F32, "guard")
+        one = held([P, 1], F32, "one")
+        eps = held([P, 1], F32, "eps")
         nc.vector.memset(big[:], 2.0 ** 80)
         nc.scalar.activation(out=big[:], in_=big[:], func=ACT.Abs_reciprocal_sqrt)
         nc.scalar.activation(out=guard[:], in_=big[:], func=ACT.Square)
         nc.vector.memset(one[:], 1.0)
         nc.vector.tensor_scalar(out=eps[:], in0=one[:], scalar1=EPS, scalar2=None, op0=ALU.mult)
 
-        steps = [keep.tile([P, T], F32, name="step%d" % j) for j in range(2)]
+        steps = [held([P, T], F32, "step%d" % j) for j in range(2)]
         for j in range(2):
             nc.vector.memset(steps[j][:], 0.0)
 
         offsets = keep.tile([P, N // 16], U16, name="offsets")
-        w_planes = [tables.tile([P, T], F32, name="w%d" % j, tag="table") for j in range(PACK)]
+        w_planes = [placed([P, T], F32, "w%d" % j, REGION * j) for j in range(PACK)]
         w_rows = wT.rearrange("(p j) c -> p j c", j=PACK)
+        weight = held([P, ROW_PASSES, PACK], F32, "weight")
+        x_raw = [[held([P, PACK, hi - lo], F32, "x_raw%d_%d" % (g, lo)) for lo, hi in X_PIECES]
+                 for g in range(ROW_PASSES)]
+        y_t = [held([P, PACK, N], F32, "y0"), placed([P, PACK, N], F32, "y1", Y1_AT)]
+        x_rows = xT[0].rearrange("(p j) r -> p j r", j=PACK)
+        y_rows = y[0].rearrange("(g p t) i -> g p t i", g=ROW_PASSES, t=PACK)
+        xm_rows = xm[0].rearrange("(g p t) d -> g p t d", g=ROW_PASSES, t=PACK)
+        xm_raw = [[held([P, PACK, 2 * P], F32, "xm_raw%d_%d" % (h, g)) for g in range(ROW_PASSES)] for h in range(2)]
+        v_planes = [held([P, T], F32, "v%d" % j) for j in range(BLOCKS)]
+        v_loaded = {0: held([P, T], F32, "v_loaded0"), 1: placed([P, T], F32, "v_loaded1", REGION * 2),
+                    3: placed([P, T], F32, "v_loaded3", REGION * 3)}
+
         nc.sync.dma_start(out=w_planes[0][:], in_=w_rows[:, 0, :])
         nc.sync.dma_start(offsets[:], offs)
         for j in range(1, PACK):
             nc.sync.dma_start(out=w_planes[j][:], in_=w_rows[:, j, :])
-        weight = keep.tile([P, ROW_PASSES, PACK], F32, name="weight")
-        x_raw = [keep.tile([P, PACK, K_PASS], F32, name="x_raw%d" % g) for g in range(ROW_PASSES)]
-        y_t = [keep.tile([P, PACK, N], F32, name="y%d" % g) for g in range(ROW_PASSES)]
-        x_rows = xT[0].rearrange("(p j) r -> p j r", j=PACK)
-        y_rows = y[0].rearrange("(g p t) i -> g p t i", g=ROW_PASSES, t=PACK)
         nc.sync.dma_start(out=weight[:], in_=wt[0].rearrange("(g p t) o -> p g (t o)", g=ROW_PASSES, t=PACK))
         for g in range(ROW_PASSES):
-            for lo, hi in X_PIECES[g]:
-                nc.sync.dma_start(out=x_raw[g][:, :, lo:hi], in_=x_rows[:, :, g * K_PASS + lo:g * K_PASS + hi])
+            for h, (lo, hi) in enumerate(X_PIECES):
+                nc.sync.dma_start(out=x_raw[g][h][:], in_=x_rows[:, :, g * K_PASS + lo:g * K_PASS + hi])
             for lo, hi in Y_PIECES[g]:
                 nc.sync.dma_start(out=y_t[g][:, lo:hi, :], in_=y_rows[g, :, lo:hi, :])
-        xm_first = keep.tile([P, ROW_PASSES, PACK, P], F32, name="xm_first", tag="slot_a", align_bytes=64)
-        xm_second = keep.tile([P, ROW_PASSES, PACK, P], F32, name="xm_second")
-        xm_rest = [keep.tile([P, PACK, D - 2 * P], F32, name="xm_rest%d" % g) for g in range(ROW_PASSES)]
-        xm_rows = xm[0].rearrange("(g p t) d -> g p t d", g=ROW_PASSES, t=PACK)
-        v_planes = [keep.tile([P, T], F32, name="v%d" % j, tag="slot_v%d" % j, align_bytes=64) for j in range(BLOCKS)]
         for g in range(ROW_PASSES):
-            nc.sync.dma_start(out=xm_first[:, g], in_=xm_rows[g, :, :, 0:P])
-        for g in range(ROW_PASSES):
-            nc.sync.dma_start(out=xm_second[:, g], in_=xm_rows[g, :, :, P:2 * P])
-        v_loaded = keep.tile([P, T], F32, name="v_loaded")
-        nc.sync.dma_start(out=v_planes[0][:], in_=vT[0:P, :])
-        nc.sync.dma_start(out=v_loaded[:], in_=vT[0:P, :])
-        nc.sync.dma_start(out=v_planes[1][:], in_=vT[P:2 * P, :])
-        for g in range(ROW_PASSES):
-            nc.sync.dma_start(out=xm_rest[g][:], in_=xm_rows[g, :, :, 2 * P:D])
-        for j in range(2, BLOCKS):
+            nc.sync.dma_start(out=xm_raw[0][g][:], in_=xm_rows[g, :, :, 0:2 * P])
+        for j in range(2):
             nc.sync.dma_start(out=v_planes[j][:], in_=vT[j * P:(j + 1) * P, :])
+        nc.sync.dma_start(out=v_loaded[0][:], in_=vT[0:P, :])
+        for g in range(ROW_PASSES):
+            nc.sync.dma_start(out=xm_raw[1][g][:], in_=xm_rows[g, :, :, 2 * P:D])
 
-        w_grouped = keep.tile([P, N, PACK], BF16, name="w_grouped", align_bytes=64)
-        for j in range(PACK):
+        w_grouped = held([P, N, PACK], BF16, "w_grouped")
+        w_codes = held([P, N], U32, "w_codes")
+        w_scales = held([P, N], U8, "w_scales")
+        for j in range(PACK - 1):
             nc.vector.tensor_copy(out=w_grouped[:, :, j], in_=w_planes[j][:].indirect(offsets[:]))
-        w_codes, w_scales = quantize("w", w_grouped[:].rearrange("p n j -> p (n j)"), E4M3)
+        halves = [slice(h * N // 2, (h + 1) * N // 2) for h in range(2)]
+        for h in range(2):
+            nc.vector.tensor_copy(out=w_grouped[:, halves[h], PACK - 1],
+                                  in_=w_planes[PACK - 1][:].indirect(offsets[:, h * N // 32:(h + 1) * N // 32]))
+        for h in range(2):
+            nc.vector.quantize_mx(out=w_codes[:, halves[h]].bitcast(E4M3), scales=w_scales[:, halves[h]],
+                                  in_=w_grouped[:, halves[h], :].rearrange("p n j -> p (n j)"))
 
-        neg_weight = keep.tile([P, ROW_PASSES, PACK], F32, name="neg_weight")
-        upper = keep.tile([P, ROW_PASSES, PACK], F32, name="upper")
-        lower = keep.tile([P, ROW_PASSES, PACK], F32, name="lower")
+        for j in (2, 3):
+            nc.sync.dma_start(out=v_planes[j][:], in_=vT[j * P:(j + 1) * P, :])
+            b = 2 * j - 3
+            nc.sync.dma_start(out=v_loaded[b][:], in_=vT[b * P:(b + 1) * P, :])
+
+        neg_weight = held([P, ROW_PASSES, PACK], F32, "neg_weight")
+        upper = held([P, ROW_PASSES, PACK], F32, "upper")
+        lower = held([P, ROW_PASSES, PACK], F32, "lower")
         nc.vector.tensor_scalar(out=neg_weight[:], in0=weight[:], scalar1=-1.0, scalar2=None, op0=ALU.mult)
         nc.vector.tensor_tensor(out=upper[:], in0=weight[:], in1=neg_weight[:], op=ALU.max)
         nc.vector.tensor_tensor(out=lower[:], in0=weight[:], in1=neg_weight[:], op=ALU.min)
 
         def first_product(g):
-            x_grouped = work.tile([P, K_PASS, PACK], BF16, name="x_grouped", align_bytes=64)
+            x_grouped = held([P, K_PASS, PACK], BF16, "x_grouped%d" % g)
             dst = x_grouped[:].rearrange("p (t m) j -> p m t j", t=PACK)
-            src = x_raw[g][:].rearrange("p j (m t) -> p m t j", t=PACK)
-            for lo, hi, on_vector in X_CASTS[g]:
-                if on_vector:
-                    nc.vector.tensor_copy(out=dst[:, lo:hi], in_=src[:, lo:hi])
-                else:
-                    nc.scalar.copy(out=dst[:, lo:hi], in_=src[:, lo:hi])
-            x_codes = keep.tile([P, K_PASS], U32, name="x_codes%d" % g, align_bytes=64)
-            x_scales = keep.tile([P, K_PASS], U8, name="x_scales%d" % g, align_bytes=64)
-            parts = 4 if g == 0 else 1
-            for c in range(parts):
-                cols = slice(c * K_PASS // parts, (c + 1) * K_PASS // parts)
+            for h, (lo, hi) in enumerate(X_PIECES):
+                cast = nc.vector.tensor_copy if (g, h) == (0, 1) else nc.scalar.copy
+                cast(out=dst[:, lo // PACK:hi // PACK], in_=x_raw[g][h][:].rearrange("p j (m t) -> p m t j", t=PACK))
+            x_codes = held([P, K_PASS], U32, "x_codes%d" % g, "y0" if g == 1 else None)
+            x_scales = held([P, K_PASS], U8, "x_scales%d" % g)
+            for cols in halves:
                 nc.vector.quantize_mx(out=x_codes[:, cols].bitcast(E4M3), scales=x_scales[:, cols],
                                       in_=x_grouped[:, cols, :].rearrange("p c j -> p (c j)"))
             banks = []
             for t in range(PACK):
-                nc.scalar.activation(out=y_t[g][:, t, :], in_=y_t[g][:, t, :], func=ACT.Copy,
-                                     scale=weight[:, g, t:t + 1])
+                if g == 0:
+                    nc.scalar.activation(out=y_t[g][:, t, :], in_=y_t[g][:, t, :], func=ACT.Copy,
+                                         scale=weight[:, g, t:t + 1])
+                else:
+                    nc.gpsimd.tensor_scalar(out=y_t[g][:, t, :], in0=y_t[g][:, t, :], scalar1=weight[:, g, t:t + 1],
+                                            scalar2=0.0, op0=ALU.mult, op1=ALU.add)
                 acc = psum.tile([P, N], F32, name="acc")
                 cols = slice(t * P, (t + 1) * P)
                 nc.tensor.matmul_mx(out=acc[:], lhsT=x_codes[:, cols].bitcast(E4M3), lhsT_scale=x_scales[:, cols],
@@ -135,7 +142,7 @@ def tile_attend_ghub_ada_kernel(tc, xT, wT, y, wt, xm, vT, offs, out_0, out_1):
             return banks
 
         def clip(g, banks):
-            clipped = work.tile([P, PACK, N], BF16, name="clipped", align_bytes=64)
+            clipped = held([P, PACK, N], BF16, "clipped%d" % g)
             for t in range(PACK):
                 nc.vector.scalar_tensor_tensor(out=y_t[g][:, t, :], in0=banks[t][:], scalar=weight[:, g, t:t + 1],
                                                in1=y_t[g][:, t, :], op0=ALU.mult, op1=ALU.subtract)
@@ -145,7 +152,7 @@ def tile_attend_ghub_ada_kernel(tc, xT, wT, y, wt, xm, vT, offs, out_0, out_1):
             return clipped
 
         def quantize_g(g, clipped):
-            g_grouped = keep.tile([P, N, PACK], BF16, name="g_grouped%d" % g, tag="slot_a" if g == 0 else "slot_g", align_bytes=64)
+            g_grouped = held([P, N, PACK], BF16, "g_grouped%d" % g)
             dst = g_grouped[:].rearrange("p (c i) t -> p c t i", i=RUN)
             src = clipped[:].rearrange("p t (c i) -> p c t i", i=RUN)
             split = IL_SPLIT[g]
@@ -153,75 +160,106 @@ def tile_attend_ghub_ada_kernel(tc, xT, wT, y, wt, xm, vT, offs, out_0, out_1):
                 nc.scalar.copy(out=dst[:, split:], in_=src[:, split:])
             if split > 0:
                 nc.vector.tensor_copy(out=dst[:, :split], in_=src[:, :split])
-            scales = keep.tile([P, N], U8, name="g_scales%d" % g, align_bytes=64)
-            nc.vector.quantize_mx(out=g_codes[:, g].bitcast(E5M2), scales=scales[:],
+            codes = placed([P, N], U32, "g_codes0", Y1_AT + 2) if g == 0 else held([P, N], U32, "g_codes1")
+            scales = held([P, N], U8, "g_scales%d" % g)
+            nc.vector.quantize_mx(out=codes[:].bitcast(E5M2), scales=scales[:],
                                   in_=g_grouped[:].rearrange("p n t -> p (n t)"))
-            return g_codes[:, g], scales
+            return codes, scales
 
-        def quantize_xm(j):
-            xm_grouped = tail.tile([P, ROW_PASSES, P, PACK], BF16, name="xm_grouped", align_bytes=64)
+        def quantize_xm(j, slot):
+            xm_grouped = held([P, ROW_PASSES, P, PACK], BF16, "xm_grouped%d" % j, slot)
             for g in range(ROW_PASSES):
-                raw = (xm_first, xm_second)[j][:, g] if j < 2 else xm_rest[g][:, :, (j - 2) * P:(j - 1) * P]
+                raw = xm_raw[j // 2][g][:, :, (j % 2) * P:(j % 2 + 1) * P]
                 nc.scalar.copy(out=xm_grouped[:, g].rearrange("p (c i) t -> p c t i", i=RUN),
                                in_=raw.rearrange("p t (c i) -> p c t i", i=RUN))
-            return quantize("xm%d" % j, xm_grouped[:].rearrange("p g d t -> p (g d t)"), E4M3)
+            if j < 2:
+                codes = placed([P, ROW_PASSES * P], U32, "xm_codes%d" % j, Y1_AT + 4 + j)
+            else:
+                codes = held([P, ROW_PASSES * P], U32, "xm_codes%d" % j)
+            scales = held([P, ROW_PASSES * P], U8, "xm_scales%d" % j)
+            nc.vector.quantize_mx(out=codes[:].bitcast(E4M3), scales=scales[:],
+                                  in_=xm_grouped[:].rearrange("p g d t -> p (g d t)"))
+            return codes, scales
 
-        def gather_v(j):
-            nv = keep.tile([P, N], F32, name="nv%d" % j, tag="slot_g" if j == 0 else "nv%d" % j, align_bytes=64)
+        def gather_v(j, slot):
+            nv = placed([P, N], F32, "nv0", Y1_AT) if j == 0 else held([P, N], F32, "nv%d" % j, slot)
             nc.vector.tensor_copy(out=nv[:], in_=v_planes[j][:].indirect(offsets[:]))
             return nv
 
         def copy_v(j):
-            v_new = tables.tile([P, T], F32, name="v_new%d" % j, tag="table")
+            v_new = placed([P, T], F32, "v_new%d" % j, REGION * (j - 1))
             for h in range(2):
                 half = slice(h * T // 2, (h + 1) * T // 2)
                 nc.scalar.activation(out=v_new[:, half], in_=v_planes[j][:, half], func=ACT.Copy)
             return v_new
 
-        clipped0 = clip(0, first_product(0))
-        banks1 = first_product(1)
-        clipped1 = clip(1, banks1)
-        xm_quant = [quantize_xm(0)]
-        g_codes = keep.tile([P, ROW_PASSES, N], U32, name="g_codes", align_bytes=64)
-        g_quant = [quantize_g(0, clipped0)]
-        g_quant.append(quantize_g(1, clipped1))
-        picked = [gather_v(0)]
-        windows = [v_loaded]
-
-        def second_product(j):
-            if j > 0:
-                xm_quant.append(quantize_xm(j))
-            xm_codes, xm_scales = xm_quant[j]
+        def second_product(j, xm_quant):
+            xm_codes, xm_scales = xm_quant
             dw = psum.tile([P, N], F32, name="dw")
             for g in range(ROW_PASSES):
                 cols = slice(g * P, (g + 1) * P)
                 nc.tensor.matmul_mx(out=dw[:], lhsT=xm_codes[:, cols].bitcast(E4M3), lhsT_scale=xm_scales[:, cols],
-                                    rhs=g_quant[g][0].bitcast(E5M2), rhs_scale=g_quant[g][1][:],
+                                    rhs=g_quant[g][0][:].bitcast(E5M2), rhs_scale=g_quant[g][1][:],
                                     start=(g == 0), stop=(g == ROW_PASSES - 1))
-            if j > 0:
-                picked.append(gather_v(j))
-            nv = picked[j]
-            inv = tail.tile([P, N], F32, name="inv")
-            nc.scalar.activation(out=inv[:], in_=dw[:], func=ACT.Square)
-            adder = nc.vector if j == 0 else nc.gpsimd
-            adder.tensor_tensor(out=nv[:], in0=picked[j][:], in1=inv[:], op=ALU.add)
-            return dw, nv, inv
+            return dw
 
-        products = [second_product(j) for j in range(BLOCKS)]
-        for j in range(BLOCKS):
-            dw, nv, inv = products[j]
-            rows = slice(j * P, (j + 1) * P)
-            if j > 0:
-                windows.append(copy_v(j))
-            v_new = windows[j]
+        def accumulate(j, dw, nv):
+            if j == 0:
+                square = held([P, N], F32, "square0")
+                descent = held([P, N], F32, "descent0")
+            elif j == 3:
+                square = held([P, N], F32, "square3", "xm_raw1_1")
+            else:
+                square = placed([P, N], F32, "square%d" % j, REGION * (j - 1) + 8)
+            nc.scalar.activation(out=square[:], in_=dw[:], func=ACT.Square)
+            adder = nc.vector if j == 0 else nc.gpsimd
+            adder.tensor_tensor(out=nv[:], in0=nv[:], in1=square[:], op=ALU.add)
+            if j == 3:
+                descent = held([P, N], F32, "descent3", "xm_raw1_1")
+            elif j > 0:
+                descent = placed([P, N], F32, "descent%d" % j, REGION * (j - 1) + 8)
+            return descent
+
+        def put_squares(j, nv, v_new):
             nc.vector.tensor_copy(out=v_new[:].indirect(offsets[:]), in_=nv[:])
-            nc.sync.dma_start(out=out_1[rows, :], in_=v_new[:])
-            descent = tail.tile([P, N], F32, name="descent")
-            nc.scalar.activation(out=inv[:], in_=nv[:], func=ACT.Abs_reciprocal_sqrt, bias=guard[:])
-            nc.scalar.activation(out=descent[:], in_=dw[:], func=ACT.Copy, scale=-LR)
-            nc.scalar.activation(out=inv[:], in_=inv[:], func=ACT.Square)
-            nc.scalar.activation(out=inv[:], in_=inv[:], func=ACT.Abs_reciprocal_sqrt)
-            nc.scalar.activation(out=inv[:], in_=inv[:], func=ACT.Square, bias=eps[:])
-            nc.scalar.activation(out=inv[:], in_=inv[:], func=ACT.Abs_reciprocal_sqrt)
+            nc.sync.dma_start(out=out_1[j * P:(j + 1) * P, :], in_=v_new[:])
+
+        def put_step(j, descent, inv):
             nc.vector.tensor_tensor(out=steps[j % 2][:].indirect(offsets[:]), in0=descent[:], in1=inv[:], op=ALU.mult)
-            nc.sync.dma_start(out=out_0[rows, :], in_=steps[j % 2][:])
+            nc.sync.dma_start(out=out_0[j * P:(j + 1) * P, :], in_=steps[j % 2][:])
+
+        def rate(j, dw, nv, descent):
+            root = held([P, N], F32, "root%d" % j, "xm_raw1_1" if j == 1 else None)
+            shifted = placed([P, N], F32, "shifted%d" % j, REGION * j + 7) if j < 2 else held([P, N], F32, "shifted%d" % j)
+            inv = held([P, N], F32, "inv%d" % j)
+            nc.scalar.activation(out=descent[:], in_=dw[:], func=ACT.Copy, scale=-LR)
+            nc.scalar.activation(out=root[:], in_=nv[:], func=ACT.Abs_reciprocal_sqrt, bias=guard[:])
+            nc.scalar.activation(out=root[:], in_=root[:], func=ACT.Square)
+            nc.scalar.activation(out=root[:], in_=root[:], func=ACT.Abs_reciprocal_sqrt)
+            nc.scalar.activation(out=shifted[:], in_=root[:], func=ACT.Square, bias=eps[:])
+            nc.scalar.activation(out=inv[:], in_=shifted[:], func=ACT.Abs_reciprocal_sqrt)
+            return inv
+
+        clipped0 = clip(0, first_product(0))
+        clipped1 = clip(1, first_product(1))
+        g_quant = [quantize_g(0, clipped0)]
+        xm_quant = [quantize_xm(0, "clipped0"), quantize_xm(1, None)]
+        picked = [gather_v(0, None)]
+        g_quant.append(quantize_g(1, clipped1))
+        picked.append(gather_v(1, "g_grouped1"))
+        products = [second_product(j, xm_quant[j]) for j in range(2)]
+        descents = [accumulate(0, products[0], picked[0])]
+        for j in range(2):
+            put_squares(j, picked[j], v_loaded[j])
+            put_step(j, descents[j], rate(j, products[j], picked[j], descents[j]))
+            if j == 0:
+                descents.append(accumulate(1, products[1], picked[1]))
+                products.extend(second_product(b, quantize_xm(b, "x_grouped%d" % (b - 2))) for b in range(2, BLOCKS))
+            picked.append(gather_v(j + 2, "inv%d" % j))
+        descents.append(accumulate(2, products[2], picked[2]))
+        put_squares(2, picked[2], copy_v(2))
+        inv2 = rate(2, products[2], picked[2], descents[2])
+        descents.append(accumulate(3, products[3], picked[3]))
+        put_squares(3, picked[3], v_loaded[3])
+        put_step(2, descents[2], inv2)
+        put_step(3, descents[3], rate(3, products[3], picked[3], descents[3]))

@@ -26,7 +26,7 @@ RUN = 4
 Y_PIECES = (((0, 1), (1, 2), (2, 4)), ((0, 2), (2, 4)))
 X_PIECES = ((0, 256), (256, 512))
 IL_SPLIT = (0, 0)
-REGION = 10
+REGION = 12
 Y1_AT = REGION * PACK
 
 
@@ -46,12 +46,10 @@ def tile_attend_ghub_ada_kernel(tc, xT, wT, y, wt, xm, vT, offs, out_0, out_1):
         big = held([P, 1], F32, "big")
         guard = held([P, 1], F32, "guard")
         one = held([P, 1], F32, "one")
-        eps = held([P, 1], F32, "eps")
         nc.vector.memset(big[:], 2.0 ** 80)
         nc.scalar.activation(out=big[:], in_=big[:], func=ACT.Abs_reciprocal_sqrt)
         nc.scalar.activation(out=guard[:], in_=big[:], func=ACT.Square)
         nc.vector.memset(one[:], 1.0)
-        nc.vector.tensor_scalar(out=eps[:], in0=one[:], scalar1=EPS, scalar2=None, op0=ALU.mult)
 
         steps = [held([P, T], F32, "step%d" % j) for j in range(2)]
         for j in range(2):
@@ -64,13 +62,13 @@ def tile_attend_ghub_ada_kernel(tc, xT, wT, y, wt, xm, vT, offs, out_0, out_1):
         x_raw = [[held([P, PACK, hi - lo], F32, "x_raw%d_%d" % (g, lo)) for lo, hi in X_PIECES]
                  for g in range(ROW_PASSES)]
         y_t = [held([P, PACK, N], F32, "y0"), placed([P, PACK, N], F32, "y1", Y1_AT)]
+        y1_raw = [held([P, 2, N], F32, "y1_raw%d" % h) for h in range(2)]
         x_rows = xT[0].rearrange("(p j) r -> p j r", j=PACK)
         y_rows = y[0].rearrange("(g p t) i -> g p t i", g=ROW_PASSES, t=PACK)
         xm_rows = xm[0].rearrange("(g p t) d -> g p t d", g=ROW_PASSES, t=PACK)
         xm_raw = [[held([P, PACK, 2 * P], F32, "xm_raw%d_%d" % (h, g)) for g in range(ROW_PASSES)] for h in range(2)]
         v_planes = [held([P, T], F32, "v%d" % j) for j in range(BLOCKS)]
-        v_loaded = {0: held([P, T], F32, "v_loaded0"), 1: placed([P, T], F32, "v_loaded1", REGION * 2),
-                    3: placed([P, T], F32, "v_loaded3", REGION * 3)}
+        v_loaded = held([P, T], F32, "v_loaded")
 
         nc.sync.dma_start(out=w_planes[0][:], in_=w_rows[:, 0, :])
         nc.sync.dma_start(offsets[:], offs)
@@ -81,14 +79,16 @@ def tile_attend_ghub_ada_kernel(tc, xT, wT, y, wt, xm, vT, offs, out_0, out_1):
             for h, (lo, hi) in enumerate(X_PIECES):
                 nc.sync.dma_start(out=x_raw[g][h][:], in_=x_rows[:, :, g * K_PASS + lo:g * K_PASS + hi])
             for lo, hi in Y_PIECES[g]:
-                nc.sync.dma_start(out=y_t[g][:, lo:hi, :], in_=y_rows[g, :, lo:hi, :])
+                nc.sync.dma_start(out=y_t[g][:, lo:hi, :] if g == 0 else y1_raw[lo // 2][:], in_=y_rows[g, :, lo:hi, :])
         for g in range(ROW_PASSES):
             nc.sync.dma_start(out=xm_raw[0][g][:], in_=xm_rows[g, :, :, 0:2 * P])
         for j in range(2):
             nc.sync.dma_start(out=v_planes[j][:], in_=vT[j * P:(j + 1) * P, :])
-        nc.sync.dma_start(out=v_loaded[0][:], in_=vT[0:P, :])
+        nc.sync.dma_start(out=v_loaded[:], in_=vT[0:P, :])
+        nc.sync.dma_start(out=v_planes[2][:], in_=vT[2 * P:3 * P, :])
         for g in range(ROW_PASSES):
             nc.sync.dma_start(out=xm_raw[1][g][:], in_=xm_rows[g, :, :, 2 * P:D])
+        nc.sync.dma_start(out=v_planes[3][:], in_=vT[3 * P:4 * P, :])
 
         w_grouped = held([P, N, PACK], BF16, "w_grouped")
         w_codes = held([P, N], U32, "w_codes")
@@ -102,11 +102,6 @@ def tile_attend_ghub_ada_kernel(tc, xT, wT, y, wt, xm, vT, offs, out_0, out_1):
         for h in range(2):
             nc.vector.quantize_mx(out=w_codes[:, halves[h]].bitcast(E4M3), scales=w_scales[:, halves[h]],
                                   in_=w_grouped[:, halves[h], :].rearrange("p n j -> p (n j)"))
-
-        for j in (2, 3):
-            nc.sync.dma_start(out=v_planes[j][:], in_=vT[j * P:(j + 1) * P, :])
-            b = 2 * j - 3
-            nc.sync.dma_start(out=v_loaded[b][:], in_=vT[b * P:(b + 1) * P, :])
 
         neg_weight = held([P, ROW_PASSES, PACK], F32, "neg_weight")
         upper = held([P, ROW_PASSES, PACK], F32, "upper")
@@ -128,12 +123,8 @@ def tile_attend_ghub_ada_kernel(tc, xT, wT, y, wt, xm, vT, offs, out_0, out_1):
                                       in_=x_grouped[:, cols, :].rearrange("p c j -> p (c j)"))
             banks = []
             for t in range(PACK):
-                if g == 0:
-                    nc.scalar.activation(out=y_t[g][:, t, :], in_=y_t[g][:, t, :], func=ACT.Copy,
-                                         scale=weight[:, g, t:t + 1])
-                else:
-                    nc.gpsimd.tensor_scalar(out=y_t[g][:, t, :], in0=y_t[g][:, t, :], scalar1=weight[:, g, t:t + 1],
-                                            scalar2=0.0, op0=ALU.mult, op1=ALU.add)
+                raw = y_t[g][:, t, :] if g == 0 else y1_raw[t // 2][:, t % 2, :]
+                nc.scalar.activation(out=y_t[g][:, t, :], in_=raw, func=ACT.Copy, scale=weight[:, g, t:t + 1])
                 acc = psum.tile([P, N], F32, name="acc")
                 cols = slice(t * P, (t + 1) * P)
                 nc.tensor.matmul_mx(out=acc[:], lhsT=x_codes[:, cols].bitcast(E4M3), lhsT_scale=x_scales[:, cols],
@@ -152,7 +143,7 @@ def tile_attend_ghub_ada_kernel(tc, xT, wT, y, wt, xm, vT, offs, out_0, out_1):
             return clipped
 
         def quantize_g(g, clipped):
-            g_grouped = held([P, N, PACK], BF16, "g_grouped%d" % g)
+            g_grouped = held([P, N, PACK], BF16, "g_grouped%d" % g, "y1_raw1" if g == 0 else None)
             dst = g_grouped[:].rearrange("p (c i) t -> p c t i", i=RUN)
             src = clipped[:].rearrange("p t (c i) -> p c t i", i=RUN)
             split = IL_SPLIT[g]
@@ -187,7 +178,10 @@ def tile_attend_ghub_ada_kernel(tc, xT, wT, y, wt, xm, vT, offs, out_0, out_1):
             return nv
 
         def copy_v(j):
-            v_new = placed([P, T], F32, "v_new%d" % j, REGION * (j - 1))
+            if j == 1:
+                v_new = held([P, T], F32, "v_new1", "xm_raw1_1")
+            else:
+                v_new = placed([P, T], F32, "v_new%d" % j, REGION * (j - 1))
             for h in range(2):
                 half = slice(h * T // 2, (h + 1) * T // 2)
                 nc.scalar.activation(out=v_new[:, half], in_=v_planes[j][:, half], func=ACT.Copy)
@@ -206,60 +200,52 @@ def tile_attend_ghub_ada_kernel(tc, xT, wT, y, wt, xm, vT, offs, out_0, out_1):
         def accumulate(j, dw, nv):
             if j == 0:
                 square = held([P, N], F32, "square0")
-                descent = held([P, N], F32, "descent0")
-            elif j == 3:
-                square = held([P, N], F32, "square3", "xm_raw1_1")
+                step = held([P, N], F32, "descent0")
             else:
                 square = placed([P, N], F32, "square%d" % j, REGION * (j - 1) + 8)
+                step = placed([P, N], F32, "descent%d" % j, REGION * (j - 1) + 10)
             nc.scalar.activation(out=square[:], in_=dw[:], func=ACT.Square)
+            nc.scalar.activation(out=step[:], in_=dw[:], func=ACT.Copy, scale=-LR)
             adder = nc.vector if j == 0 else nc.gpsimd
             adder.tensor_tensor(out=nv[:], in0=nv[:], in1=square[:], op=ALU.add)
-            if j == 3:
-                descent = held([P, N], F32, "descent3", "xm_raw1_1")
-            elif j > 0:
-                descent = placed([P, N], F32, "descent%d" % j, REGION * (j - 1) + 8)
-            return descent
+            return step
 
         def put_squares(j, nv, v_new):
             nc.vector.tensor_copy(out=v_new[:].indirect(offsets[:]), in_=nv[:])
             nc.sync.dma_start(out=out_1[j * P:(j + 1) * P, :], in_=v_new[:])
 
-        def put_step(j, descent, inv):
-            nc.vector.tensor_tensor(out=steps[j % 2][:].indirect(offsets[:]), in0=descent[:], in1=inv[:], op=ALU.mult)
-            nc.sync.dma_start(out=out_0[j * P:(j + 1) * P, :], in_=steps[j % 2][:])
-
-        def rate(j, dw, nv, descent):
-            root = held([P, N], F32, "root%d" % j, "xm_raw1_1" if j == 1 else None)
-            shifted = placed([P, N], F32, "shifted%d" % j, REGION * j + 7) if j < 2 else held([P, N], F32, "shifted%d" % j)
+        def put_step(j, step, nv):
+            root = held([P, N], F32, "root%d" % j, "v1" if j == 1 else None)
+            shifted = placed([P, 5 * N // 2], F32, "shifted%d" % j, REGION * j + 7)
             inv = held([P, N], F32, "inv%d" % j)
-            nc.scalar.activation(out=descent[:], in_=dw[:], func=ACT.Copy, scale=-LR)
             nc.scalar.activation(out=root[:], in_=nv[:], func=ACT.Abs_reciprocal_sqrt, bias=guard[:])
-            nc.scalar.activation(out=root[:], in_=root[:], func=ACT.Square)
-            nc.scalar.activation(out=root[:], in_=root[:], func=ACT.Abs_reciprocal_sqrt)
-            nc.scalar.activation(out=shifted[:], in_=root[:], func=ACT.Square, bias=eps[:])
-            nc.scalar.activation(out=inv[:], in_=shifted[:], func=ACT.Abs_reciprocal_sqrt)
-            return inv
+            nc.scalar.activation(out=shifted[:, 0:N], in_=root[:], func=ACT.Abs_reciprocal_sqrt, scale=EPS, bias=one[:])
+            nc.scalar.activation(out=inv[:], in_=shifted[:, 0:N], func=ACT.Square)
+            nc.gpsimd.tensor_tensor(out=step[:], in0=step[:], in1=root[:], op=ALU.mult)
+            nc.gpsimd.tensor_tensor(out=step[:], in0=step[:], in1=inv[:], op=ALU.mult)
+            nc.vector.tensor_copy(out=steps[j % 2][:].indirect(offsets[:]), in_=step[:])
+            nc.sync.dma_start(out=out_0[j * P:(j + 1) * P, :], in_=steps[j % 2][:])
 
         clipped0 = clip(0, first_product(0))
         clipped1 = clip(1, first_product(1))
         g_quant = [quantize_g(0, clipped0)]
-        xm_quant = [quantize_xm(0, "clipped0"), quantize_xm(1, None)]
+        xm_quant = [quantize_xm(0, "clipped0")]
         picked = [gather_v(0, None)]
         g_quant.append(quantize_g(1, clipped1))
         picked.append(gather_v(1, "g_grouped1"))
+        xm_quant.append(quantize_xm(1, "clipped1"))
         products = [second_product(j, xm_quant[j]) for j in range(2)]
-        descents = [accumulate(0, products[0], picked[0])]
-        for j in range(2):
-            put_squares(j, picked[j], v_loaded[j])
-            put_step(j, descents[j], rate(j, products[j], picked[j], descents[j]))
+        step = accumulate(0, products[0], picked[0])
+        window = v_loaded
+        for j in range(BLOCKS):
+            put_squares(j, picked[j], window)
             if j == 0:
-                descents.append(accumulate(1, products[1], picked[1]))
+                picked.append(gather_v(2, None))
+            put_step(j, step, picked[j])
+            if j + 1 < BLOCKS:
+                step = accumulate(j + 1, products[j + 1], picked[j + 1])
+            if j == 0:
                 products.extend(second_product(b, quantize_xm(b, "x_grouped%d" % (b - 2))) for b in range(2, BLOCKS))
-            picked.append(gather_v(j + 2, "inv%d" % j))
-        descents.append(accumulate(2, products[2], picked[2]))
-        put_squares(2, picked[2], copy_v(2))
-        inv2 = rate(2, products[2], picked[2], descents[2])
-        descents.append(accumulate(3, products[3], picked[3]))
-        put_squares(3, picked[3], v_loaded[3])
-        put_step(2, descents[2], inv2)
-        put_step(3, descents[3], rate(3, products[3], picked[3], descents[3]))
+                picked.append(gather_v(3, None))
+            if j + 1 < BLOCKS:
+                window = copy_v(j + 1)

@@ -26,6 +26,7 @@ RUN = 4
 Y_PIECES = (((0, 1), (1, 2), (2, 4)), ((0, 2), (2, 4)))
 X_PIECES = ((0, 256), (256, 512))
 IL_SPLIT = (0, 0)
+X_ON_VECTOR = 44
 REGION = 12
 Y1_AT = REGION * PACK
 
@@ -61,7 +62,10 @@ def tile_attend_ghub_ada_kernel(tc, xT, wT, y, wt, xm, vT, offs, out_0, out_1):
         weight = held([P, ROW_PASSES, PACK], F32, "weight")
         x_raw = [[held([P, PACK, hi - lo], F32, "x_raw%d_%d" % (g, lo)) for lo, hi in X_PIECES]
                  for g in range(ROW_PASSES)]
-        y_t = [held([P, PACK, N], F32, "y0"), placed([P, PACK, N], F32, "y1", Y1_AT)]
+        y0 = held([P, PACK, N], F32, "y0")
+        y1_head = placed([P, PACK - 1, N], F32, "y1_head", Y1_AT)
+        y1_last = held([P, N], F32, "y1_last")
+        y_t = [[y0[:, t, :] for t in range(PACK)], [y1_head[:, t, :] for t in range(PACK - 1)] + [y1_last[:]]]
         y1_raw = [held([P, 2, N], F32, "y1_raw%d" % h) for h in range(2)]
         x_rows = xT[0].rearrange("(p j) r -> p j r", j=PACK)
         y_rows = y[0].rearrange("(g p t) i -> g p t i", g=ROW_PASSES, t=PACK)
@@ -74,12 +78,12 @@ def tile_attend_ghub_ada_kernel(tc, xT, wT, y, wt, xm, vT, offs, out_0, out_1):
         nc.sync.dma_start(offsets[:], offs)
         for j in range(1, PACK):
             nc.sync.dma_start(out=w_planes[j][:], in_=w_rows[:, j, :])
-        nc.sync.dma_start(out=weight[:], in_=wt[0].rearrange("(g p t) o -> p g (t o)", g=ROW_PASSES, t=PACK))
+        nc.scalar.dma_start(out=weight[:], in_=wt[0].rearrange("(g p t) o -> p g (t o)", g=ROW_PASSES, t=PACK))
         for g in range(ROW_PASSES):
             for h, (lo, hi) in enumerate(X_PIECES):
                 nc.sync.dma_start(out=x_raw[g][h][:], in_=x_rows[:, :, g * K_PASS + lo:g * K_PASS + hi])
             for lo, hi in Y_PIECES[g]:
-                nc.sync.dma_start(out=y_t[g][:, lo:hi, :] if g == 0 else y1_raw[lo // 2][:], in_=y_rows[g, :, lo:hi, :])
+                nc.sync.dma_start(out=y0[:, lo:hi, :] if g == 0 else y1_raw[lo // 2][:], in_=y_rows[g, :, lo:hi, :])
         for g in range(ROW_PASSES):
             nc.sync.dma_start(out=xm_raw[0][g][:], in_=xm_rows[g, :, :, 0:2 * P])
         for j in range(2):
@@ -112,19 +116,22 @@ def tile_attend_ghub_ada_kernel(tc, xT, wT, y, wt, xm, vT, offs, out_0, out_1):
 
         def first_product(g):
             x_grouped = held([P, K_PASS, PACK], BF16, "x_grouped%d" % g)
-            dst = x_grouped[:].rearrange("p (t m) j -> p m t j", t=PACK)
+            dst = x_grouped[:].rearrange("p (t m) j -> p m j t", t=PACK)
             for h, (lo, hi) in enumerate(X_PIECES):
-                cast = nc.vector.tensor_copy if (g, h) == (0, 1) else nc.scalar.copy
-                cast(out=dst[:, lo // PACK:hi // PACK], in_=x_raw[g][h][:].rearrange("p j (m t) -> p m t j", t=PACK))
-            x_codes = held([P, K_PASS], U32, "x_codes%d" % g, "y0" if g == 1 else None)
+                src = x_raw[g][h][:].rearrange("p j (m t) -> p m j t", t=PACK)
+                split = X_ON_VECTOR if (g, h) == (0, 1) else 0
+                if split > 0:
+                    nc.vector.tensor_copy(out=dst[:, lo // PACK:lo // PACK + split], in_=src[:, :split])
+                nc.scalar.copy(out=dst[:, lo // PACK + split:hi // PACK], in_=src[:, split:])
+            x_codes = held([P, K_PASS], U32, "x_codes%d" % g)
             x_scales = held([P, K_PASS], U8, "x_scales%d" % g)
-            for cols in halves:
+            for cols in (slice(0, P), slice(P, 2 * P), slice(2 * P, 4 * P)):
                 nc.vector.quantize_mx(out=x_codes[:, cols].bitcast(E4M3), scales=x_scales[:, cols],
                                       in_=x_grouped[:, cols, :].rearrange("p c j -> p (c j)"))
             banks = []
             for t in range(PACK):
-                raw = y_t[g][:, t, :] if g == 0 else y1_raw[t // 2][:, t % 2, :]
-                nc.scalar.activation(out=y_t[g][:, t, :], in_=raw, func=ACT.Copy, scale=weight[:, g, t:t + 1])
+                raw = y_t[g][t] if g == 0 else y1_raw[t // 2][:, t % 2, :]
+                nc.scalar.activation(out=y_t[g][t], in_=raw, func=ACT.Copy, scale=weight[:, g, t:t + 1])
                 acc = psum.tile([P, N], F32, name="acc")
                 cols = slice(t * P, (t + 1) * P)
                 nc.tensor.matmul_mx(out=acc[:], lhsT=x_codes[:, cols].bitcast(E4M3), lhsT_scale=x_scales[:, cols],
@@ -133,12 +140,15 @@ def tile_attend_ghub_ada_kernel(tc, xT, wT, y, wt, xm, vT, offs, out_0, out_1):
             return banks
 
         def clip(g, banks):
-            clipped = held([P, PACK, N], BF16, "clipped%d" % g)
+            if g == 0:
+                clipped = held([P, PACK, N], BF16, "clipped0")
+            else:
+                clipped = placed([P, PACK, N], BF16, "clipped1", Y1_AT + 6)
             for t in range(PACK):
-                nc.vector.scalar_tensor_tensor(out=y_t[g][:, t, :], in0=banks[t][:], scalar=weight[:, g, t:t + 1],
-                                               in1=y_t[g][:, t, :], op0=ALU.mult, op1=ALU.subtract)
+                nc.vector.scalar_tensor_tensor(out=y_t[g][t], in0=banks[t][:], scalar=weight[:, g, t:t + 1],
+                                               in1=y_t[g][t], op0=ALU.mult, op1=ALU.subtract)
             for t in range(PACK):
-                nc.vector.tensor_scalar(out=clipped[:, t, :], in0=y_t[g][:, t, :], scalar1=lower[:, g, t:t + 1],
+                nc.vector.tensor_scalar(out=clipped[:, t, :], in0=y_t[g][t], scalar1=lower[:, g, t:t + 1],
                                         scalar2=upper[:, g, t:t + 1], op0=ALU.max, op1=ALU.min)
             return clipped
 
@@ -158,7 +168,10 @@ def tile_attend_ghub_ada_kernel(tc, xT, wT, y, wt, xm, vT, offs, out_0, out_1):
             return codes, scales
 
         def quantize_xm(j, slot):
-            xm_grouped = held([P, ROW_PASSES, P, PACK], BF16, "xm_grouped%d" % j, slot)
+            if j == 1:
+                xm_grouped = placed([P, ROW_PASSES, P, PACK], BF16, "xm_grouped1", Y1_AT + 6)
+            else:
+                xm_grouped = held([P, ROW_PASSES, P, PACK], BF16, "xm_grouped%d" % j, slot)
             for g in range(ROW_PASSES):
                 raw = xm_raw[j // 2][g][:, :, (j % 2) * P:(j % 2 + 1) * P]
                 nc.scalar.copy(out=xm_grouped[:, g].rearrange("p (c i) t -> p c t i", i=RUN),
@@ -173,7 +186,7 @@ def tile_attend_ghub_ada_kernel(tc, xT, wT, y, wt, xm, vT, offs, out_0, out_1):
             return codes, scales
 
         def gather_v(j, slot):
-            nv = placed([P, N], F32, "nv0", Y1_AT) if j == 0 else held([P, N], F32, "nv%d" % j, slot)
+            nv = placed([P, N], F32, "nv%d" % j, Y1_AT + 8 * j) if j < 2 else held([P, N], F32, "nv%d" % j, slot)
             nc.vector.tensor_copy(out=nv[:], in_=v_planes[j][:].indirect(offsets[:]))
             return nv
 
@@ -246,6 +259,6 @@ def tile_attend_ghub_ada_kernel(tc, xT, wT, y, wt, xm, vT, offs, out_0, out_1):
                 step = accumulate(j + 1, products[j + 1], picked[j + 1])
             if j == 0:
                 products.extend(second_product(b, quantize_xm(b, "x_grouped%d" % (b - 2))) for b in range(2, BLOCKS))
-                picked.append(gather_v(3, None))
+                picked.append(gather_v(3, "x_grouped0"))
             if j + 1 < BLOCKS:
                 window = copy_v(j + 1)

@@ -23,7 +23,7 @@ K_PASS = P * PACK
 ROW_PASSES = R // K_PASS
 BLOCKS = D // P
 RUN = 4
-Y_PIECES = (((0, 1), (1, 2), (2, 4)), ((0, 2), (2, 4)))
+Y_PIECES = (((0, 1), (1, 2), (2, 4)), ((0, 2), (2, 3), (3, 4)))
 X_PIECES = ((0, 256), (256, 512))
 IL_SPLIT = (0, 0)
 X_ON_VECTOR = 44
@@ -66,13 +66,13 @@ def tile_attend_ghub_ada_kernel(tc, xT, wT, y, wt, xm, vT, offs, out_0, out_1):
         y1_head = placed([P, PACK - 1, N], F32, "y1_head", Y1_AT)
         y1_last = held([P, N], F32, "y1_last")
         y_t = [[y0[:, t, :] for t in range(PACK)], [y1_head[:, t, :] for t in range(PACK - 1)] + [y1_last[:]]]
-        y1_raw = [held([P, 2, N], F32, "y1_raw%d" % h) for h in range(2)]
+        y1_raw = [held([P, hi - lo, N], F32, "y1_raw%d" % lo) for lo, hi in Y_PIECES[1]]
+        y1_rows = [y1_raw[0][:, 0, :], y1_raw[0][:, 1, :], y1_raw[1][:, 0, :], y1_raw[2][:, 0, :]]
         x_rows = xT[0].rearrange("(p j) r -> p j r", j=PACK)
         y_rows = y[0].rearrange("(g p t) i -> g p t i", g=ROW_PASSES, t=PACK)
         xm_rows = xm[0].rearrange("(g p t) d -> g p t d", g=ROW_PASSES, t=PACK)
         xm_raw = [[held([P, PACK, 2 * P], F32, "xm_raw%d_%d" % (h, g)) for g in range(ROW_PASSES)] for h in range(2)]
         v_planes = [held([P, T], F32, "v%d" % j) for j in range(BLOCKS)]
-        v_loaded = held([P, T], F32, "v_loaded")
 
         nc.sync.dma_start(out=w_planes[0][:], in_=w_rows[:, 0, :])
         nc.sync.dma_start(offsets[:], offs)
@@ -82,14 +82,12 @@ def tile_attend_ghub_ada_kernel(tc, xT, wT, y, wt, xm, vT, offs, out_0, out_1):
         for g in range(ROW_PASSES):
             for h, (lo, hi) in enumerate(X_PIECES):
                 nc.sync.dma_start(out=x_raw[g][h][:], in_=x_rows[:, :, g * K_PASS + lo:g * K_PASS + hi])
-            for lo, hi in Y_PIECES[g]:
-                nc.sync.dma_start(out=y0[:, lo:hi, :] if g == 0 else y1_raw[lo // 2][:], in_=y_rows[g, :, lo:hi, :])
+            for h, (lo, hi) in enumerate(Y_PIECES[g]):
+                nc.sync.dma_start(out=y0[:, lo:hi, :] if g == 0 else y1_raw[h][:], in_=y_rows[g, :, lo:hi, :])
         for g in range(ROW_PASSES):
             nc.sync.dma_start(out=xm_raw[0][g][:], in_=xm_rows[g, :, :, 0:2 * P])
-        for j in range(2):
+        for j in range(3):
             nc.sync.dma_start(out=v_planes[j][:], in_=vT[j * P:(j + 1) * P, :])
-        nc.sync.dma_start(out=v_loaded[:], in_=vT[0:P, :])
-        nc.sync.dma_start(out=v_planes[2][:], in_=vT[2 * P:3 * P, :])
         for g in range(ROW_PASSES):
             nc.sync.dma_start(out=xm_raw[1][g][:], in_=xm_rows[g, :, :, 2 * P:D])
         nc.sync.dma_start(out=v_planes[3][:], in_=vT[3 * P:4 * P, :])
@@ -130,7 +128,7 @@ def tile_attend_ghub_ada_kernel(tc, xT, wT, y, wt, xm, vT, offs, out_0, out_1):
                                       in_=x_grouped[:, cols, :].rearrange("p c j -> p (c j)"))
             banks = []
             for t in range(PACK):
-                raw = y_t[g][t] if g == 0 else y1_raw[t // 2][:, t % 2, :]
+                raw = y_t[g][t] if g == 0 else y1_rows[t]
                 nc.scalar.activation(out=y_t[g][t], in_=raw, func=ACT.Copy, scale=weight[:, g, t:t + 1])
                 acc = psum.tile([P, N], F32, name="acc")
                 cols = slice(t * P, (t + 1) * P)
@@ -152,8 +150,8 @@ def tile_attend_ghub_ada_kernel(tc, xT, wT, y, wt, xm, vT, offs, out_0, out_1):
                                         scalar2=upper[:, g, t:t + 1], op0=ALU.max, op1=ALU.min)
             return clipped
 
-        def quantize_g(g, clipped):
-            g_grouped = held([P, N, PACK], BF16, "g_grouped%d" % g, "y1_raw1" if g == 0 else None)
+        def interleave_g(g, clipped):
+            g_grouped = held([P, N, PACK], BF16, "g_grouped%d" % g, "y1_raw3" if g == 0 else None)
             dst = g_grouped[:].rearrange("p (c i) t -> p c t i", i=RUN)
             src = clipped[:].rearrange("p t (c i) -> p c t i", i=RUN)
             split = IL_SPLIT[g]
@@ -161,37 +159,40 @@ def tile_attend_ghub_ada_kernel(tc, xT, wT, y, wt, xm, vT, offs, out_0, out_1):
                 nc.scalar.copy(out=dst[:, split:], in_=src[:, split:])
             if split > 0:
                 nc.vector.tensor_copy(out=dst[:, :split], in_=src[:, :split])
-            codes = placed([P, N], U32, "g_codes0", Y1_AT + 2) if g == 0 else held([P, N], U32, "g_codes1")
+            return g_grouped
+
+        def quantize_g(g, g_grouped):
+            codes = placed([P, N], U32, "g_codes%d" % g, Y1_AT + 2 + 2 * g)
             scales = held([P, N], U8, "g_scales%d" % g)
             nc.vector.quantize_mx(out=codes[:].bitcast(E5M2), scales=scales[:],
                                   in_=g_grouped[:].rearrange("p n t -> p (n t)"))
             return codes, scales
 
         def quantize_xm(j, slot):
-            if j == 1:
-                xm_grouped = placed([P, ROW_PASSES, P, PACK], BF16, "xm_grouped1", Y1_AT + 6)
+            if j < 2:
+                xm_grouped = placed([P, ROW_PASSES, P, PACK], BF16, "xm_grouped%d" % j, Y1_AT + 4 + 2 * j)
             else:
                 xm_grouped = held([P, ROW_PASSES, P, PACK], BF16, "xm_grouped%d" % j, slot)
             for g in range(ROW_PASSES):
                 raw = xm_raw[j // 2][g][:, :, (j % 2) * P:(j % 2 + 1) * P]
-                nc.scalar.copy(out=xm_grouped[:, g].rearrange("p (c i) t -> p c t i", i=RUN),
+                cast = nc.vector.tensor_copy if j == 0 else nc.scalar.copy
+                cast(out=xm_grouped[:, g].rearrange("p (c i) t -> p c t i", i=RUN),
                                in_=raw.rearrange("p t (c i) -> p c t i", i=RUN))
-            if j < 2:
-                codes = placed([P, ROW_PASSES * P], U32, "xm_codes%d" % j, Y1_AT + 4 + j)
-            else:
-                codes = held([P, ROW_PASSES * P], U32, "xm_codes%d" % j)
+            codes = held([P, ROW_PASSES * P], U32, "xm_codes%d" % j)
             scales = held([P, ROW_PASSES * P], U8, "xm_scales%d" % j)
             nc.vector.quantize_mx(out=codes[:].bitcast(E4M3), scales=scales[:],
                                   in_=xm_grouped[:].rearrange("p g d t -> p (g d t)"))
             return codes, scales
 
         def gather_v(j, slot):
-            nv = placed([P, N], F32, "nv%d" % j, Y1_AT + 8 * j) if j < 2 else held([P, N], F32, "nv%d" % j, slot)
+            nv = placed([P, N], F32, "nv%d" % j, Y1_AT) if j == 0 else held([P, N], F32, "nv%d" % j, slot)
             nc.vector.tensor_copy(out=nv[:], in_=v_planes[j][:].indirect(offsets[:]))
             return nv
 
         def copy_v(j):
-            if j == 1:
+            if j == 0:
+                v_new = placed([P, T], F32, "v_new0", Y1_AT + 9)
+            elif j == 1:
                 v_new = held([P, T], F32, "v_new1", "xm_raw1_1")
             else:
                 v_new = placed([P, T], F32, "v_new%d" % j, REGION * (j - 1))
@@ -241,19 +242,20 @@ def tile_attend_ghub_ada_kernel(tc, xT, wT, y, wt, xm, vT, offs, out_0, out_1):
 
         clipped0 = clip(0, first_product(0))
         clipped1 = clip(1, first_product(1))
-        g_quant = [quantize_g(0, clipped0)]
+        g_quant = [quantize_g(0, interleave_g(0, clipped0))]
         xm_quant = [quantize_xm(0, "clipped0")]
+        g_grouped1 = interleave_g(1, clipped1)
         picked = [gather_v(0, None)]
-        g_quant.append(quantize_g(1, clipped1))
+        g_quant.append(quantize_g(1, g_grouped1))
         picked.append(gather_v(1, "g_grouped1"))
-        xm_quant.append(quantize_xm(1, "clipped1"))
+        xm_quant.append(quantize_xm(1, None))
         products = [second_product(j, xm_quant[j]) for j in range(2)]
+        window = copy_v(0)
         step = accumulate(0, products[0], picked[0])
-        window = v_loaded
         for j in range(BLOCKS):
             put_squares(j, picked[j], window)
             if j == 0:
-                picked.append(gather_v(2, None))
+                picked.append(gather_v(2, "square0"))
             put_step(j, step, picked[j])
             if j + 1 < BLOCKS:
                 step = accumulate(j + 1, products[j + 1], picked[j + 1])

@@ -23,9 +23,11 @@ K_PASS = P * PACK
 ROW_PASSES = R // K_PASS
 BLOCKS = D // P
 RUN = 4
-Y_PIECES = (((0, 1), (1, 2), (2, 4)), ((0, 2), (2, 3), (3, 4)))
+Y_PIECES = (((0, 1), (1, 2), (2, 3), (3, 4)), ((0, 1), (1, 2), (2, 3), (3, 4)))
+CLIPS_ON_GPSIMD = (4, 2)
+X_ON_VECTOR1 = 64
 X_PIECES = ((0, 256), (256, 512))
-IL_SPLIT = (0, 0)
+IL_SPLIT = (0, 128)
 X_ON_VECTOR = 44
 REGION = 12
 Y1_AT = REGION * PACK
@@ -67,7 +69,7 @@ def tile_attend_ghub_ada_kernel(tc, xT, wT, y, wt, xm, vT, offs, out_0, out_1):
         y1_last = held([P, N], F32, "y1_last")
         y_t = [[y0[:, t, :] for t in range(PACK)], [y1_head[:, t, :] for t in range(PACK - 1)] + [y1_last[:]]]
         y1_raw = [held([P, hi - lo, N], F32, "y1_raw%d" % lo) for lo, hi in Y_PIECES[1]]
-        y1_rows = [y1_raw[0][:, 0, :], y1_raw[0][:, 1, :], y1_raw[1][:, 0, :], y1_raw[2][:, 0, :]]
+        y1_rows = [raw[:, 0, :] for raw in y1_raw]
         x_rows = xT[0].rearrange("(p j) r -> p j r", j=PACK)
         y_rows = y[0].rearrange("(g p t) i -> g p t i", g=ROW_PASSES, t=PACK)
         xm_rows = xm[0].rearrange("(g p t) d -> g p t d", g=ROW_PASSES, t=PACK)
@@ -79,11 +81,23 @@ def tile_attend_ghub_ada_kernel(tc, xT, wT, y, wt, xm, vT, offs, out_0, out_1):
         for j in range(1, PACK):
             nc.sync.dma_start(out=w_planes[j][:], in_=w_rows[:, j, :])
         nc.scalar.dma_start(out=weight[:], in_=wt[0].rearrange("(g p t) o -> p g (t o)", g=ROW_PASSES, t=PACK))
-        for g in range(ROW_PASSES):
-            for h, (lo, hi) in enumerate(X_PIECES):
-                nc.sync.dma_start(out=x_raw[g][h][:], in_=x_rows[:, :, g * K_PASS + lo:g * K_PASS + hi])
-            for h, (lo, hi) in enumerate(Y_PIECES[g]):
-                nc.sync.dma_start(out=y0[:, lo:hi, :] if g == 0 else y1_raw[h][:], in_=y_rows[g, :, lo:hi, :])
+        def load_x(g, h):
+            lo, hi = X_PIECES[h]
+            nc.sync.dma_start(out=x_raw[g][h][:], in_=x_rows[:, :, g * K_PASS + lo:g * K_PASS + hi])
+
+        def load_y(g, h):
+            lo, hi = Y_PIECES[g][h]
+            nc.sync.dma_start(out=y0[:, lo:hi, :] if g == 0 else y1_raw[h][:], in_=y_rows[g, :, lo:hi, :])
+
+        load_x(0, 0)
+        load_x(0, 1)
+        for h in range(2):
+            load_y(0, h)
+            load_x(1, h)
+        for h in range(2, PACK):
+            load_y(0, h)
+        for h in range(PACK):
+            load_y(1, h)
         for g in range(ROW_PASSES):
             nc.sync.dma_start(out=xm_raw[0][g][:], in_=xm_rows[g, :, :, 0:2 * P])
         for j in range(3):
@@ -112,20 +126,25 @@ def tile_attend_ghub_ada_kernel(tc, xT, wT, y, wt, xm, vT, offs, out_0, out_1):
         nc.vector.tensor_tensor(out=upper[:], in0=weight[:], in1=neg_weight[:], op=ALU.max)
         nc.vector.tensor_tensor(out=lower[:], in0=weight[:], in1=neg_weight[:], op=ALU.min)
 
-        def first_product(g):
+        def quantize_x(g):
             x_grouped = held([P, K_PASS, PACK], BF16, "x_grouped%d" % g)
             dst = x_grouped[:].rearrange("p (t m) j -> p m j t", t=PACK)
             for h, (lo, hi) in enumerate(X_PIECES):
                 src = x_raw[g][h][:].rearrange("p j (m t) -> p m j t", t=PACK)
-                split = X_ON_VECTOR if (g, h) == (0, 1) else 0
+                split = (X_ON_VECTOR, X_ON_VECTOR1)[g] if h == 1 else 0
                 if split > 0:
                     nc.vector.tensor_copy(out=dst[:, lo // PACK:lo // PACK + split], in_=src[:, :split])
-                nc.scalar.copy(out=dst[:, lo // PACK + split:hi // PACK], in_=src[:, split:])
+                if split < (hi - lo) // PACK:
+                    nc.scalar.copy(out=dst[:, lo // PACK + split:hi // PACK], in_=src[:, split:])
             x_codes = held([P, K_PASS], U32, "x_codes%d" % g)
             x_scales = held([P, K_PASS], U8, "x_scales%d" % g)
             for cols in (slice(0, P), slice(P, 2 * P), slice(2 * P, 4 * P)):
                 nc.vector.quantize_mx(out=x_codes[:, cols].bitcast(E4M3), scales=x_scales[:, cols],
                                       in_=x_grouped[:, cols, :].rearrange("p c j -> p (c j)"))
+            return x_codes, x_scales
+
+        def first_product(g, x_quant):
+            x_codes, x_scales = x_quant
             banks = []
             for t in range(PACK):
                 raw = y_t[g][t] if g == 0 else y1_rows[t]
@@ -146,8 +165,9 @@ def tile_attend_ghub_ada_kernel(tc, xT, wT, y, wt, xm, vT, offs, out_0, out_1):
                 nc.vector.scalar_tensor_tensor(out=y_t[g][t], in0=banks[t][:], scalar=weight[:, g, t:t + 1],
                                                in1=y_t[g][t], op0=ALU.mult, op1=ALU.subtract)
             for t in range(PACK):
-                nc.vector.tensor_scalar(out=clipped[:, t, :], in0=y_t[g][t], scalar1=lower[:, g, t:t + 1],
-                                        scalar2=upper[:, g, t:t + 1], op0=ALU.max, op1=ALU.min)
+                engine = nc.gpsimd if t < CLIPS_ON_GPSIMD[g] else nc.vector
+                engine.tensor_scalar(out=clipped[:, t, :], in0=y_t[g][t], scalar1=upper[:, g, t:t + 1],
+                                     scalar2=lower[:, g, t:t + 1], op0=ALU.min, op1=ALU.max)
             return clipped
 
         def interleave_g(g, clipped):
@@ -162,20 +182,18 @@ def tile_attend_ghub_ada_kernel(tc, xT, wT, y, wt, xm, vT, offs, out_0, out_1):
             return g_grouped
 
         def quantize_g(g, g_grouped):
-            codes = placed([P, N], U32, "g_codes%d" % g, Y1_AT + 2 + 2 * g)
+            codes = placed([P, N], U32, "g_codes0", Y1_AT + 2) if g == 0 else held([P, N], U32, "g_codes1")
             scales = held([P, N], U8, "g_scales%d" % g)
             nc.vector.quantize_mx(out=codes[:].bitcast(E5M2), scales=scales[:],
                                   in_=g_grouped[:].rearrange("p n t -> p (n t)"))
             return codes, scales
 
         def quantize_xm(j, slot):
-            if j < 2:
-                xm_grouped = placed([P, ROW_PASSES, P, PACK], BF16, "xm_grouped%d" % j, Y1_AT + 4 + 2 * j)
-            else:
+            if True:
                 xm_grouped = held([P, ROW_PASSES, P, PACK], BF16, "xm_grouped%d" % j, slot)
             for g in range(ROW_PASSES):
                 raw = xm_raw[j // 2][g][:, :, (j % 2) * P:(j % 2 + 1) * P]
-                cast = nc.vector.tensor_copy if j == 0 else nc.scalar.copy
+                cast = nc.scalar.copy
                 cast(out=xm_grouped[:, g].rearrange("p (c i) t -> p c t i", i=RUN),
                                in_=raw.rearrange("p t (c i) -> p c t i", i=RUN))
             codes = held([P, ROW_PASSES * P], U32, "xm_codes%d" % j)
@@ -185,13 +203,13 @@ def tile_attend_ghub_ada_kernel(tc, xT, wT, y, wt, xm, vT, offs, out_0, out_1):
             return codes, scales
 
         def gather_v(j, slot):
-            nv = placed([P, N], F32, "nv%d" % j, Y1_AT) if j == 0 else held([P, N], F32, "nv%d" % j, slot)
+            nv = held([P, N], F32, "nv%d" % j, slot)
             nc.vector.tensor_copy(out=nv[:], in_=v_planes[j][:].indirect(offsets[:]))
             return nv
 
         def copy_v(j):
             if j == 0:
-                v_new = placed([P, T], F32, "v_new0", Y1_AT + 9)
+                v_new = held([P, T], F32, "v_new0")
             elif j == 1:
                 v_new = held([P, T], F32, "v_new1", "xm_raw1_1")
             else:
@@ -240,17 +258,16 @@ def tile_attend_ghub_ada_kernel(tc, xT, wT, y, wt, xm, vT, offs, out_0, out_1):
             nc.vector.tensor_copy(out=steps[j % 2][:].indirect(offsets[:]), in_=step[:])
             nc.sync.dma_start(out=out_0[j * P:(j + 1) * P, :], in_=steps[j % 2][:])
 
-        clipped0 = clip(0, first_product(0))
-        clipped1 = clip(1, first_product(1))
-        g_quant = [quantize_g(0, interleave_g(0, clipped0))]
+        x_quant = [quantize_x(g) for g in range(ROW_PASSES)]
+        clipped0 = clip(0, first_product(0, x_quant[0]))
+        clipped1 = clip(1, first_product(1, x_quant[1]))
+        g_grouped = [interleave_g(0, clipped0), interleave_g(1, clipped1)]
+        g_quant = [quantize_g(g, g_grouped[g]) for g in range(ROW_PASSES)]
         xm_quant = [quantize_xm(0, "clipped0")]
-        g_grouped1 = interleave_g(1, clipped1)
-        picked = [gather_v(0, None)]
-        g_quant.append(quantize_g(1, g_grouped1))
-        picked.append(gather_v(1, "g_grouped1"))
+        picked = [gather_v(0, "g_grouped1"), gather_v(1, None)]
+        window = copy_v(0)
         xm_quant.append(quantize_xm(1, None))
         products = [second_product(j, xm_quant[j]) for j in range(2)]
-        window = copy_v(0)
         step = accumulate(0, products[0], picked[0])
         for j in range(BLOCKS):
             put_squares(j, picked[j], window)

@@ -31,6 +31,7 @@ IL_SPLIT = (0, 128)
 X_ON_VECTOR = 44
 REGION = 12
 Y1_AT = REGION * PACK
+LATE_AT = Y1_AT + 10
 
 
 def tile_attend_ghub_ada_kernel(tc, xT, wT, y, wt, xm, vT, offs, out_0, out_1):
@@ -44,7 +45,7 @@ def tile_attend_ghub_ada_kernel(tc, xT, wT, y, wt, xm, vT, offs, out_0, out_1):
             return keep.tile(shape, dtype, name=name, tag=slot or name, align_bytes=64)
 
         def placed(shape, dtype, name, kib):
-            return handed.tile(shape, dtype, name=name, offset=kib * 1024, align_bytes=64)
+            return handed.tile(shape, dtype, name=name, offset=int(kib * 1024), align_bytes=64)
 
         big = held([P, 1], F32, "big")
         guard = held([P, 1], F32, "guard")
@@ -100,8 +101,11 @@ def tile_attend_ghub_ada_kernel(tc, xT, wT, y, wt, xm, vT, offs, out_0, out_1):
             load_y(1, h)
         for g in range(ROW_PASSES):
             nc.sync.dma_start(out=xm_raw[0][g][:], in_=xm_rows[g, :, :, 0:2 * P])
-        for j in range(3):
+        for j in range(2):
             nc.sync.dma_start(out=v_planes[j][:], in_=vT[j * P:(j + 1) * P, :])
+        window1 = placed([P, T], F32, "v_new1", REGION)
+        nc.sync.dma_start(out=window1[:, T // 2:T], in_=vT[P:2 * P, T // 2:T])
+        nc.sync.dma_start(out=v_planes[2][:], in_=vT[2 * P:3 * P, :])
         for g in range(ROW_PASSES):
             nc.sync.dma_start(out=xm_raw[1][g][:], in_=xm_rows[g, :, :, 2 * P:D])
         nc.sync.dma_start(out=v_planes[3][:], in_=vT[3 * P:4 * P, :])
@@ -188,38 +192,34 @@ def tile_attend_ghub_ada_kernel(tc, xT, wT, y, wt, xm, vT, offs, out_0, out_1):
                                   in_=g_grouped[:].rearrange("p n t -> p (n t)"))
             return codes, scales
 
-        def quantize_xm(j, slot):
-            if True:
-                xm_grouped = held([P, ROW_PASSES, P, PACK], BF16, "xm_grouped%d" % j, slot)
+        def interleave_xm(first, count, xm_grouped):
             for g in range(ROW_PASSES):
-                raw = xm_raw[j // 2][g][:, :, (j % 2) * P:(j % 2 + 1) * P]
-                cast = nc.scalar.copy
-                cast(out=xm_grouped[:, g].rearrange("p (c i) t -> p c t i", i=RUN),
-                               in_=raw.rearrange("p t (c i) -> p c t i", i=RUN))
-            codes = held([P, ROW_PASSES * P], U32, "xm_codes%d" % j)
-            scales = held([P, ROW_PASSES * P], U8, "xm_scales%d" % j)
-            nc.vector.quantize_mx(out=codes[:].bitcast(E4M3), scales=scales[:],
-                                  in_=xm_grouped[:].rearrange("p g d t -> p (g d t)"))
-            return codes, scales
+                for b in range(count):
+                    j = first + b
+                    raw = xm_raw[j // 2][g][:, :, (j % 2) * P:(j % 2 + 1) * P]
+                    nc.scalar.copy(out=xm_grouped[:, b, g].rearrange("p (c i) t -> p c t i", i=RUN),
+                                   in_=raw.rearrange("p t (c i) -> p c t i", i=RUN))
+            return xm_grouped
 
-        def gather_v(j, slot):
-            nv = held([P, N], F32, "nv%d" % j, slot)
+        def quantize_xm(first, count, xm_grouped, scales):
+            codes = held([P, count, ROW_PASSES * P], U32, "xm_codes%d" % first)
+            nc.vector.quantize_mx(out=codes[:].rearrange("p b c -> p (b c)").bitcast(E4M3),
+                                  scales=scales[:].rearrange("p b c -> p (b c)"),
+                                  in_=xm_grouped[:].rearrange("p b g d t -> p (b g d t)"))
+            return [(codes[:, b, :], scales[:, b, :]) for b in range(count)]
+
+        def gather_v(j, nv):
             nc.vector.tensor_copy(out=nv[:], in_=v_planes[j][:].indirect(offsets[:]))
             return nv
 
         def copy_v(j):
-            if j == 0:
-                v_new = held([P, T], F32, "v_new0")
-            elif j == 1:
-                v_new = held([P, T], F32, "v_new1", "xm_raw1_1")
-            else:
-                v_new = placed([P, T], F32, "v_new%d" % j, REGION * (j - 1))
-            for h in range(2):
+            v_new = window1 if j == 1 else placed([P, T], F32, "v_new%d" % j, REGION * j)
+            for h in range(1 if j == 1 else 2):
                 half = slice(h * T // 2, (h + 1) * T // 2)
                 nc.scalar.activation(out=v_new[:, half], in_=v_planes[j][:, half], func=ACT.Copy)
             return v_new
 
-        def second_product(j, xm_quant):
+        def second_product(xm_quant):
             xm_codes, xm_scales = xm_quant
             dw = psum.tile([P, N], F32, name="dw")
             for g in range(ROW_PASSES):
@@ -229,32 +229,36 @@ def tile_attend_ghub_ada_kernel(tc, xT, wT, y, wt, xm, vT, offs, out_0, out_1):
                                     start=(g == 0), stop=(g == ROW_PASSES - 1))
             return dw
 
-        def accumulate(j, dw, nv):
-            if j == 0:
-                square = held([P, N], F32, "square0")
-                step = held([P, N], F32, "descent0")
-            else:
-                square = placed([P, N], F32, "square%d" % j, REGION * (j - 1) + 8)
-                step = placed([P, N], F32, "descent%d" % j, REGION * (j - 1) + 10)
+        def add_square(j, dw, nv):
+            square = held([P, N], F32, "square%d" % j, "square%d" % (j % 2))
             nc.scalar.activation(out=square[:], in_=dw[:], func=ACT.Square)
-            nc.scalar.activation(out=step[:], in_=dw[:], func=ACT.Copy, scale=-LR)
             adder = nc.vector if j == 0 else nc.gpsimd
             adder.tensor_tensor(out=nv[:], in0=nv[:], in1=square[:], op=ALU.add)
+
+        def scale_dw(j, dw):
+            step = held([P, N], F32, "descent%d" % j)
+            nc.scalar.activation(out=step[:], in_=dw[:], func=ACT.Copy, scale=-LR)
             return step
 
         def put_squares(j, nv, v_new):
             nc.vector.tensor_copy(out=v_new[:].indirect(offsets[:]), in_=nv[:])
             nc.sync.dma_start(out=out_1[j * P:(j + 1) * P, :], in_=v_new[:])
 
-        def put_step(j, step, nv):
-            root = held([P, N], F32, "root%d" % j, "v1" if j == 1 else None)
-            shifted = placed([P, 5 * N // 2], F32, "shifted%d" % j, REGION * j + 7)
-            inv = held([P, N], F32, "inv%d" % j)
+        def divide(j, step, nv):
+            root = held([P, N], F32, "root%d" % j, ("root0", "xm_raw1_0", "root0", "root3")[j])
+            if j == 1:
+                shifted = placed([P, N], F32, "shifted1", REGION * 2)
+                inv = placed([P, N], F32, "inv1", LATE_AT + 1.5)
+            else:
+                shifted = held([P, N], F32, "shifted%d" % j, "shifted")
+                inv = held([P, N], F32, "inv%d" % j, "inv%d" % (j % 2))
             nc.scalar.activation(out=root[:], in_=nv[:], func=ACT.Abs_reciprocal_sqrt, bias=guard[:])
-            nc.scalar.activation(out=shifted[:, 0:N], in_=root[:], func=ACT.Abs_reciprocal_sqrt, scale=EPS, bias=one[:])
-            nc.scalar.activation(out=inv[:], in_=shifted[:, 0:N], func=ACT.Square)
+            nc.scalar.activation(out=shifted[:], in_=root[:], func=ACT.Abs_reciprocal_sqrt, scale=EPS, bias=one[:])
+            nc.scalar.activation(out=inv[:], in_=shifted[:], func=ACT.Square)
             nc.gpsimd.tensor_tensor(out=step[:], in0=step[:], in1=root[:], op=ALU.mult)
             nc.gpsimd.tensor_tensor(out=step[:], in0=step[:], in1=inv[:], op=ALU.mult)
+
+        def put_step(j, step):
             nc.vector.tensor_copy(out=steps[j % 2][:].indirect(offsets[:]), in_=step[:])
             nc.sync.dma_start(out=out_0[j * P:(j + 1) * P, :], in_=steps[j % 2][:])
 
@@ -263,21 +267,39 @@ def tile_attend_ghub_ada_kernel(tc, xT, wT, y, wt, xm, vT, offs, out_0, out_1):
         clipped1 = clip(1, first_product(1, x_quant[1]))
         g_grouped = [interleave_g(0, clipped0), interleave_g(1, clipped1)]
         g_quant = [quantize_g(g, g_grouped[g]) for g in range(ROW_PASSES)]
-        xm_quant = [quantize_xm(0, "clipped0")]
-        picked = [gather_v(0, "g_grouped1"), gather_v(1, None)]
-        window = copy_v(0)
-        xm_quant.append(quantize_xm(1, None))
-        products = [second_product(j, xm_quant[j]) for j in range(2)]
-        step = accumulate(0, products[0], picked[0])
-        for j in range(BLOCKS):
-            put_squares(j, picked[j], window)
-            if j == 0:
-                picked.append(gather_v(2, "square0"))
-            put_step(j, step, picked[j])
-            if j + 1 < BLOCKS:
-                step = accumulate(j + 1, products[j + 1], picked[j + 1])
-            if j == 0:
-                products.extend(second_product(b, quantize_xm(b, "x_grouped%d" % (b - 2))) for b in range(2, BLOCKS))
-                picked.append(gather_v(3, "x_grouped0"))
-            if j + 1 < BLOCKS:
-                window = copy_v(j + 1)
+        def early_xm(j, slot):
+            grouped = interleave_xm(j, 1, held([P, 1, ROW_PASSES, P, PACK], BF16, "xm_grouped%d" % j, slot))
+            return quantize_xm(j, 1, grouped, held([P, 1, ROW_PASSES * P], U8, "xm_scales%d" % j))
+
+        xm_quant = early_xm(0, "clipped0")
+        picked = [gather_v(0, held([P, N], F32, "nv0", "g_grouped1")), gather_v(1, held([P, N], F32, "nv1"))]
+        windows = [copy_v(0)]
+        xm_quant.extend(early_xm(1, None))
+        products = [second_product(xm_quant[j]) for j in range(2)]
+        add_square(0, products[0], picked[0])
+        scaled = [scale_dw(0, products[0])]
+        add_square(1, products[1], picked[1])
+        windows.append(copy_v(1))
+        for j in range(2):
+            put_squares(j, picked[j], windows[j])
+        divide(0, scaled[0], picked[0])
+        put_step(0, scaled[0])
+        rest = interleave_xm(2, 2, placed([P, 2, ROW_PASSES, P, PACK], BF16, "xm_grouped2", REGION * 3))
+        scaled.append(scale_dw(1, products[1]))
+        divide(1, scaled[1], picked[1])
+        xm_quant.extend(quantize_xm(2, 2, rest, placed([P, 2, ROW_PASSES * P], U8, "xm_scales2", LATE_AT + 2)))
+        late3 = gather_v(3, placed([P, N], F32, "nv3", LATE_AT))
+        picked.extend([gather_v(2, placed([P, N], F32, "nv2", LATE_AT + 2.5)), late3])
+        put_step(1, scaled[1])
+        windows.append(copy_v(2))
+        products.extend(second_product(xm_quant[j]) for j in range(2, BLOCKS))
+        for j in range(2, BLOCKS):
+            add_square(j, products[j], picked[j])
+        windows.append(copy_v(3))
+        for j in range(2, BLOCKS):
+            scaled.append(scale_dw(j, products[j]))
+        for j in range(2, BLOCKS):
+            put_squares(j, picked[j], windows[j])
+        for j in range(2, BLOCKS):
+            divide(j, scaled[j], picked[j])
+            put_step(j, scaled[j])

@@ -23,15 +23,11 @@ K_PASS = P * PACK
 ROW_PASSES = R // K_PASS
 BLOCKS = D // P
 RUN = 4
-Y_PIECES = (((0, 1), (1, 2), (2, 3), (3, 4)), ((0, 1), (1, 2), (2, 3), (3, 4)))
 CLIPS_ON_GPSIMD = (4, 2)
-X_ON_VECTOR1 = 64
 X_PIECES = ((0, 256), (256, 512))
-IL_SPLIT = (0, 128)
-X_ON_VECTOR = 44
-REGION = 12
-Y1_AT = REGION * PACK
-LATE_AT = Y1_AT + 10
+X_ON_VECTOR = (44, 64)
+PLANE_KIB = 8
+Y1_AT = PLANE_KIB * PACK
 
 
 def tile_attend_ghub_ada_kernel(tc, xT, wT, y, wt, xm, vT, offs, out_0, out_1):
@@ -45,7 +41,7 @@ def tile_attend_ghub_ada_kernel(tc, xT, wT, y, wt, xm, vT, offs, out_0, out_1):
             return keep.tile(shape, dtype, name=name, tag=slot or name, align_bytes=64)
 
         def placed(shape, dtype, name, kib):
-            return handed.tile(shape, dtype, name=name, offset=int(kib * 1024), align_bytes=64)
+            return handed.tile(shape, dtype, name=name, offset=kib * 1024, align_bytes=64)
 
         big = held([P, 1], F32, "big")
         guard = held([P, 1], F32, "guard")
@@ -55,12 +51,12 @@ def tile_attend_ghub_ada_kernel(tc, xT, wT, y, wt, xm, vT, offs, out_0, out_1):
         nc.scalar.activation(out=guard[:], in_=big[:], func=ACT.Square)
         nc.vector.memset(one[:], 1.0)
 
-        steps = [held([P, T], F32, "step%d" % j) for j in range(2)]
-        for j in range(2):
-            nc.vector.memset(steps[j][:], 0.0)
+        step_windows = [held([P, T], F32, "step_window%d" % j) for j in range(BLOCKS)]
+        for j in range(BLOCKS):
+            (nc.vector if j < 2 else nc.gpsimd).memset(step_windows[j][:], 0.0)
 
         offsets = keep.tile([P, N // 16], U16, name="offsets")
-        w_planes = [placed([P, T], F32, "w%d" % j, REGION * j) for j in range(PACK)]
+        w_planes = [placed([P, T], F32, "w%d" % j, PLANE_KIB * j) for j in range(PACK)]
         w_rows = wT.rearrange("(p j) c -> p j c", j=PACK)
         weight = held([P, ROW_PASSES, PACK], F32, "weight")
         x_raw = [[held([P, PACK, hi - lo], F32, "x_raw%d_%d" % (g, lo)) for lo, hi in X_PIECES]
@@ -69,8 +65,7 @@ def tile_attend_ghub_ada_kernel(tc, xT, wT, y, wt, xm, vT, offs, out_0, out_1):
         y1_head = placed([P, PACK - 1, N], F32, "y1_head", Y1_AT)
         y1_last = held([P, N], F32, "y1_last")
         y_t = [[y0[:, t, :] for t in range(PACK)], [y1_head[:, t, :] for t in range(PACK - 1)] + [y1_last[:]]]
-        y1_raw = [held([P, hi - lo, N], F32, "y1_raw%d" % lo) for lo, hi in Y_PIECES[1]]
-        y1_rows = [raw[:, 0, :] for raw in y1_raw]
+        y1_raw = [held([P, N], F32, "y1_raw%d" % t) for t in range(PACK)]
         x_rows = xT[0].rearrange("(p j) r -> p j r", j=PACK)
         y_rows = y[0].rearrange("(g p t) i -> g p t i", g=ROW_PASSES, t=PACK)
         xm_rows = xm[0].rearrange("(g p t) d -> g p t d", g=ROW_PASSES, t=PACK)
@@ -82,43 +77,48 @@ def tile_attend_ghub_ada_kernel(tc, xT, wT, y, wt, xm, vT, offs, out_0, out_1):
         for j in range(1, PACK):
             nc.sync.dma_start(out=w_planes[j][:], in_=w_rows[:, j, :])
         nc.scalar.dma_start(out=weight[:], in_=wt[0].rearrange("(g p t) o -> p g (t o)", g=ROW_PASSES, t=PACK))
+
         def load_x(g, h):
             lo, hi = X_PIECES[h]
             nc.sync.dma_start(out=x_raw[g][h][:], in_=x_rows[:, :, g * K_PASS + lo:g * K_PASS + hi])
 
-        def load_y(g, h):
-            lo, hi = Y_PIECES[g][h]
-            nc.sync.dma_start(out=y0[:, lo:hi, :] if g == 0 else y1_raw[h][:], in_=y_rows[g, :, lo:hi, :])
+        def load_y(g, t):
+            nc.sync.dma_start(out=y0[:, t, :] if g == 0 else y1_raw[t][:], in_=y_rows[g, :, t, :])
+
+        def load_xm(h):
+            for g in range(ROW_PASSES):
+                nc.sync.dma_start(out=xm_raw[h][g][:], in_=xm_rows[g, :, :, 2 * h * P:2 * (h + 1) * P])
+
+        def load_v(j, tile):
+            nc.sync.dma_start(out=tile[:], in_=vT[j * P:(j + 1) * P, :])
 
         load_x(0, 0)
         load_x(0, 1)
         for h in range(2):
             load_y(0, h)
             load_x(1, h)
-        for h in range(2, PACK):
-            load_y(0, h)
-        for h in range(PACK):
-            load_y(1, h)
-        for g in range(ROW_PASSES):
-            nc.sync.dma_start(out=xm_raw[0][g][:], in_=xm_rows[g, :, :, 0:2 * P])
-        for j in range(2):
-            nc.sync.dma_start(out=v_planes[j][:], in_=vT[j * P:(j + 1) * P, :])
-        window1 = placed([P, T], F32, "v_new1", REGION)
-        nc.sync.dma_start(out=window1[:, T // 2:T], in_=vT[P:2 * P, T // 2:T])
-        nc.sync.dma_start(out=v_planes[2][:], in_=vT[2 * P:3 * P, :])
-        for g in range(ROW_PASSES):
-            nc.sync.dma_start(out=xm_raw[1][g][:], in_=xm_rows[g, :, :, 2 * P:D])
-        nc.sync.dma_start(out=v_planes[3][:], in_=vT[3 * P:4 * P, :])
+        for t in range(2, PACK):
+            load_y(0, t)
+        for t in range(PACK):
+            load_y(1, t)
+        load_xm(0)
+        for j in range(3):
+            load_v(j, v_planes[j])
+        load_xm(1)
+        load_v(3, v_planes[3])
+        v_windows = [placed([P, T], F32, "v_window%d" % j, PLANE_KIB * j) for j in range(BLOCKS)]
+        load_v(3, v_windows[3])
 
         w_grouped = held([P, N, PACK], BF16, "w_grouped")
         w_codes = held([P, N], U32, "w_codes")
         w_scales = held([P, N], U8, "w_scales")
+        halves = [slice(h * N // 2, (h + 1) * N // 2) for h in range(2)]
+        half_lists = [offsets[:, h * N // 32:(h + 1) * N // 32] for h in range(2)]
         for j in range(PACK - 1):
             nc.vector.tensor_copy(out=w_grouped[:, :, j], in_=w_planes[j][:].indirect(offsets[:]))
-        halves = [slice(h * N // 2, (h + 1) * N // 2) for h in range(2)]
         for h in range(2):
             nc.vector.tensor_copy(out=w_grouped[:, halves[h], PACK - 1],
-                                  in_=w_planes[PACK - 1][:].indirect(offsets[:, h * N // 32:(h + 1) * N // 32]))
+                                  in_=w_planes[PACK - 1][:].indirect(half_lists[h]))
         for h in range(2):
             nc.vector.quantize_mx(out=w_codes[:, halves[h]].bitcast(E4M3), scales=w_scales[:, halves[h]],
                                   in_=w_grouped[:, halves[h], :].rearrange("p n j -> p (n j)"))
@@ -135,7 +135,7 @@ def tile_attend_ghub_ada_kernel(tc, xT, wT, y, wt, xm, vT, offs, out_0, out_1):
             dst = x_grouped[:].rearrange("p (t m) j -> p m j t", t=PACK)
             for h, (lo, hi) in enumerate(X_PIECES):
                 src = x_raw[g][h][:].rearrange("p j (m t) -> p m j t", t=PACK)
-                split = (X_ON_VECTOR, X_ON_VECTOR1)[g] if h == 1 else 0
+                split = X_ON_VECTOR[g] if h == 1 else 0
                 if split > 0:
                     nc.vector.tensor_copy(out=dst[:, lo // PACK:lo // PACK + split], in_=src[:, :split])
                 if split < (hi - lo) // PACK:
@@ -151,7 +151,7 @@ def tile_attend_ghub_ada_kernel(tc, xT, wT, y, wt, xm, vT, offs, out_0, out_1):
             x_codes, x_scales = x_quant
             banks = []
             for t in range(PACK):
-                raw = y_t[g][t] if g == 0 else y1_rows[t]
+                raw = y_t[g][t] if g == 0 else y1_raw[t][:]
                 nc.scalar.activation(out=y_t[g][t], in_=raw, func=ACT.Copy, scale=weight[:, g, t:t + 1])
                 acc = psum.tile([P, N], F32, name="acc")
                 cols = slice(t * P, (t + 1) * P)
@@ -164,7 +164,7 @@ def tile_attend_ghub_ada_kernel(tc, xT, wT, y, wt, xm, vT, offs, out_0, out_1):
             if g == 0:
                 clipped = held([P, PACK, N], BF16, "clipped0")
             else:
-                clipped = placed([P, PACK, N], BF16, "clipped1", Y1_AT + 6)
+                clipped = held([P, PACK, N], BF16, "clipped1")
             for t in range(PACK):
                 nc.vector.scalar_tensor_tensor(out=y_t[g][t], in0=banks[t][:], scalar=weight[:, g, t:t + 1],
                                                in1=y_t[g][t], op0=ALU.mult, op1=ALU.subtract)
@@ -178,11 +178,10 @@ def tile_attend_ghub_ada_kernel(tc, xT, wT, y, wt, xm, vT, offs, out_0, out_1):
             g_grouped = held([P, N, PACK], BF16, "g_grouped%d" % g, "y1_raw3" if g == 0 else None)
             dst = g_grouped[:].rearrange("p (c i) t -> p c t i", i=RUN)
             src = clipped[:].rearrange("p t (c i) -> p c t i", i=RUN)
-            split = IL_SPLIT[g]
-            if split < N // RUN:
-                nc.scalar.copy(out=dst[:, split:], in_=src[:, split:])
-            if split > 0:
-                nc.vector.tensor_copy(out=dst[:, :split], in_=src[:, :split])
+            if g == 0:
+                nc.scalar.copy(out=dst, in_=src)
+            else:
+                nc.vector.tensor_copy(out=dst, in_=src)
             return g_grouped
 
         def quantize_g(g, g_grouped):
@@ -192,32 +191,27 @@ def tile_attend_ghub_ada_kernel(tc, xT, wT, y, wt, xm, vT, offs, out_0, out_1):
                                   in_=g_grouped[:].rearrange("p n t -> p (n t)"))
             return codes, scales
 
-        def interleave_xm(first, count, xm_grouped):
+        def interleave_xm(first, count, slot, on_vector):
+            grouped = held([P, count, ROW_PASSES, P, PACK], BF16, "xm_grouped%d" % first, slot)
             for g in range(ROW_PASSES):
                 for b in range(count):
                     j = first + b
                     raw = xm_raw[j // 2][g][:, :, (j % 2) * P:(j % 2 + 1) * P]
-                    nc.scalar.copy(out=xm_grouped[:, b, g].rearrange("p (c i) t -> p c t i", i=RUN),
-                                   in_=raw.rearrange("p t (c i) -> p c t i", i=RUN))
-            return xm_grouped
+                    dst = grouped[:, b, g].rearrange("p (c i) t -> p c t i", i=RUN)
+                    src = raw.rearrange("p t (c i) -> p c t i", i=RUN)
+                    if on_vector:
+                        nc.vector.tensor_copy(out=dst, in_=src)
+                    else:
+                        nc.scalar.copy(out=dst, in_=src)
+            return grouped
 
-        def quantize_xm(first, count, xm_grouped, scales):
+        def quantize_xm(first, count, grouped):
             codes = held([P, count, ROW_PASSES * P], U32, "xm_codes%d" % first)
+            scales = held([P, count, ROW_PASSES * P], U8, "xm_scales%d" % first)
             nc.vector.quantize_mx(out=codes[:].rearrange("p b c -> p (b c)").bitcast(E4M3),
                                   scales=scales[:].rearrange("p b c -> p (b c)"),
-                                  in_=xm_grouped[:].rearrange("p b g d t -> p (b g d t)"))
+                                  in_=grouped[:].rearrange("p b g d t -> p (b g d t)"))
             return [(codes[:, b, :], scales[:, b, :]) for b in range(count)]
-
-        def gather_v(j, nv):
-            nc.vector.tensor_copy(out=nv[:], in_=v_planes[j][:].indirect(offsets[:]))
-            return nv
-
-        def copy_v(j):
-            v_new = window1 if j == 1 else placed([P, T], F32, "v_new%d" % j, REGION * j)
-            for h in range(1 if j == 1 else 2):
-                half = slice(h * T // 2, (h + 1) * T // 2)
-                nc.scalar.activation(out=v_new[:, half], in_=v_planes[j][:, half], func=ACT.Copy)
-            return v_new
 
         def second_product(xm_quant):
             xm_codes, xm_scales = xm_quant
@@ -229,77 +223,75 @@ def tile_attend_ghub_ada_kernel(tc, xT, wT, y, wt, xm, vT, offs, out_0, out_1):
                                     start=(g == 0), stop=(g == ROW_PASSES - 1))
             return dw
 
+        def gather_v(j):
+            nv = held([P, N], F32, "nv%d" % j, "nv1" if j == 3 else None)
+            nc.scalar.activation(out=nv[:], in_=v_planes[j][:].indirect(offsets[:]), func=ACT.Copy)
+            return nv
+
+        def copy_v(j):
+            nc.vector.tensor_copy(out=v_windows[j][:], in_=v_planes[j][:])
+
         def add_square(j, dw, nv):
-            square = held([P, N], F32, "square%d" % j, "square%d" % (j % 2))
+            square = held([P, N], F32, "square%d" % j)
             nc.scalar.activation(out=square[:], in_=dw[:], func=ACT.Square)
             adder = nc.vector if j == 0 else nc.gpsimd
             adder.tensor_tensor(out=nv[:], in0=nv[:], in1=square[:], op=ALU.add)
 
-        def scale_dw(j, dw):
-            step = held([P, N], F32, "descent%d" % j)
-            nc.scalar.activation(out=step[:], in_=dw[:], func=ACT.Copy, scale=-LR)
-            return step
+        def roots(j, nv):
+            root = held([P, N], F32, "root%d" % j, "v3" if j == 2 else None)
+            shifted = held([P, N], F32, "shifted%d" % j)
+            factor = held([P, N], F32, "factor%d" % j, "shifted%d" % (j - 1) if j % 2 else "square%d" % (j + 1))
+            for half in halves:
+                nc.scalar.activation(out=root[:, half], in_=nv[:, half], func=ACT.Abs_reciprocal_sqrt, bias=guard[:])
+            for half in halves:
+                nc.scalar.activation(out=shifted[:, half], in_=root[:, half], func=ACT.Abs_reciprocal_sqrt,
+                                     scale=EPS, bias=one[:])
+            nc.gpsimd.tensor_tensor(out=factor[:], in0=root[:], in1=shifted[:], op=ALU.mult)
+            nc.gpsimd.tensor_tensor(out=factor[:], in0=factor[:], in1=shifted[:], op=ALU.mult)
+            return factor
 
-        def put_squares(j, nv, v_new):
-            nc.vector.tensor_copy(out=v_new[:].indirect(offsets[:]), in_=nv[:])
-            nc.sync.dma_start(out=out_1[j * P:(j + 1) * P, :], in_=v_new[:])
-
-        def divide(j, step, nv):
-            root = held([P, N], F32, "root%d" % j, ("root0", "xm_raw1_0", "root0", "root3")[j])
-            if j == 1:
-                shifted = placed([P, N], F32, "shifted1", REGION * 2)
-                inv = placed([P, N], F32, "inv1", LATE_AT + 1.5)
+        def put_squares(j, nv):
+            if j == 0:
+                nc.vector.tensor_copy(out=v_windows[j][:].indirect(offsets[:]), in_=nv[:])
             else:
-                shifted = held([P, N], F32, "shifted%d" % j, "shifted")
-                inv = held([P, N], F32, "inv%d" % j, "inv%d" % (j % 2))
-            nc.scalar.activation(out=root[:], in_=nv[:], func=ACT.Abs_reciprocal_sqrt, bias=guard[:])
-            nc.scalar.activation(out=shifted[:], in_=root[:], func=ACT.Abs_reciprocal_sqrt, scale=EPS, bias=one[:])
-            nc.scalar.activation(out=inv[:], in_=shifted[:], func=ACT.Square)
-            nc.gpsimd.tensor_tensor(out=step[:], in0=step[:], in1=root[:], op=ALU.mult)
-            nc.gpsimd.tensor_tensor(out=step[:], in0=step[:], in1=inv[:], op=ALU.mult)
+                for h in range(2):
+                    nc.scalar.activation(out=v_windows[j][:].indirect(half_lists[h]), in_=nv[:, halves[h]],
+                                         func=ACT.Copy)
+            nc.sync.dma_start(out=out_1[j * P:(j + 1) * P, :], in_=v_windows[j][:])
 
-        def put_step(j, step):
-            nc.vector.tensor_copy(out=steps[j % 2][:].indirect(offsets[:]), in_=step[:])
-            nc.sync.dma_start(out=out_0[j * P:(j + 1) * P, :], in_=steps[j % 2][:])
+        def put_step(j, dw, factor):
+            step = held([P, N], F32, "step%d" % j, "xm_grouped2")
+            nc.vector.scalar_tensor_tensor(out=step[:], in0=dw[:], scalar=-LR, in1=factor[:],
+                                           op0=ALU.mult, op1=ALU.mult)
+            nc.vector.tensor_copy(out=step_windows[j][:].indirect(offsets[:]), in_=step[:])
+            nc.sync.dma_start(out=out_0[j * P:(j + 1) * P, :], in_=step_windows[j][:])
 
         x_quant = [quantize_x(g) for g in range(ROW_PASSES)]
         clipped0 = clip(0, first_product(0, x_quant[0]))
         clipped1 = clip(1, first_product(1, x_quant[1]))
         g_grouped = [interleave_g(0, clipped0), interleave_g(1, clipped1)]
         g_quant = [quantize_g(g, g_grouped[g]) for g in range(ROW_PASSES)]
-        def early_xm(j, slot):
-            grouped = interleave_xm(j, 1, held([P, 1, ROW_PASSES, P, PACK], BF16, "xm_grouped%d" % j, slot))
-            return quantize_xm(j, 1, grouped, held([P, 1, ROW_PASSES * P], U8, "xm_scales%d" % j))
-
-        xm_quant = early_xm(0, "clipped0")
-        picked = [gather_v(0, held([P, N], F32, "nv0", "g_grouped1")), gather_v(1, held([P, N], F32, "nv1"))]
-        windows = [copy_v(0)]
-        xm_quant.extend(early_xm(1, None))
+        xm_quant = quantize_xm(0, 1, interleave_xm(0, 1, "clipped0", False))
+        xm_quant.extend(quantize_xm(1, 1, interleave_xm(1, 1, None, False)))
         products = [second_product(xm_quant[j]) for j in range(2)]
-        add_square(0, products[0], picked[0])
-        scaled = [scale_dw(0, products[0])]
-        add_square(1, products[1], picked[1])
-        windows.append(copy_v(1))
+        picked = []
         for j in range(2):
-            put_squares(j, picked[j], windows[j])
-        divide(0, scaled[0], picked[0])
-        put_step(0, scaled[0])
-        rest = interleave_xm(2, 2, placed([P, 2, ROW_PASSES, P, PACK], BF16, "xm_grouped2", REGION * 3))
-        scaled.append(scale_dw(1, products[1]))
-        divide(1, scaled[1], picked[1])
-        xm_quant.extend(quantize_xm(2, 2, rest, placed([P, 2, ROW_PASSES * P], U8, "xm_scales2", LATE_AT + 2)))
-        late3 = gather_v(3, placed([P, N], F32, "nv3", LATE_AT))
-        picked.extend([gather_v(2, placed([P, N], F32, "nv2", LATE_AT + 2.5)), late3])
-        put_step(1, scaled[1])
-        windows.append(copy_v(2))
+            picked.append(gather_v(j))
+            copy_v(j)
+            add_square(j, products[j], picked[j])
+        factors = [roots(j, picked[j]) for j in range(2)]
+        put_squares(0, picked[0])
+        copy_v(2)
+        picked.append(gather_v(2))
+        put_squares(1, picked[1])
+        xm_quant.extend(quantize_xm(2, 2, interleave_xm(2, 2, None, True)))
         products.extend(second_product(xm_quant[j]) for j in range(2, BLOCKS))
+        picked.append(gather_v(3))
+        for j in range(2):
+            put_step(j, products[j], factors[j])
         for j in range(2, BLOCKS):
             add_square(j, products[j], picked[j])
-        windows.append(copy_v(3))
+        factors.extend(roots(j, picked[j]) for j in range(2, BLOCKS))
         for j in range(2, BLOCKS):
-            scaled.append(scale_dw(j, products[j]))
-        for j in range(2, BLOCKS):
-            put_squares(j, picked[j], windows[j])
-        for j in range(2, BLOCKS):
-            divide(j, scaled[j], picked[j])
-            put_step(j, scaled[j])
+            put_squares(j, picked[j])
+            put_step(j, products[j], factors[j])

@@ -51,9 +51,9 @@ def tile_attend_ghub_ada_kernel(tc, xT, wT, y, wt, xm, vT, offs, out_0, out_1):
         nc.scalar.activation(out=guard[:], in_=big[:], func=ACT.Square)
         nc.vector.memset(one[:], 1.0)
 
-        step_windows = [held([P, T], F32, "step_window%d" % j) for j in range(BLOCKS)]
-        for j in range(BLOCKS):
-            (nc.vector if j < 2 else nc.gpsimd).memset(step_windows[j][:], 0.0)
+        step_windows = [held([P, T], F32, "step_window%d" % j) for j in range(2)]
+        for j in range(2):
+            nc.vector.memset(step_windows[j][:], 0.0)
 
         offsets = keep.tile([P, N // 16], U16, name="offsets")
         w_planes = [placed([P, T], F32, "w%d" % j, PLANE_KIB * j) for j in range(PACK)]
@@ -263,8 +263,8 @@ def tile_attend_ghub_ada_kernel(tc, xT, wT, y, wt, xm, vT, offs, out_0, out_1):
             step = held([P, N], F32, "step%d" % j, "xm_grouped2")
             nc.vector.scalar_tensor_tensor(out=step[:], in0=dw[:], scalar=-LR, in1=factor[:],
                                            op0=ALU.mult, op1=ALU.mult)
-            nc.vector.tensor_copy(out=step_windows[j][:].indirect(offsets[:]), in_=step[:])
-            nc.sync.dma_start(out=out_0[j * P:(j + 1) * P, :], in_=step_windows[j][:])
+            nc.vector.tensor_copy(out=step_windows[j % 2][:].indirect(offsets[:]), in_=step[:])
+            nc.sync.dma_start(out=out_0[j * P:(j + 1) * P, :], in_=step_windows[j % 2][:])
 
         x_quant = [quantize_x(g) for g in range(ROW_PASSES)]
         clipped0 = clip(0, first_product(0, x_quant[0]))

@@ -102,11 +102,13 @@ def tile_attend_ghub_ada_kernel(tc, xT, wT, y, wt, xm, vT, offs, out_0, out_1):
         for t in range(PACK):
             load_y(1, t)
         load_xm(0)
-        for j in range(3):
+        v_windows = [placed([P, T], F32, "v_window%d" % j, PLANE_KIB * j) for j in range(BLOCKS)]
+        for j in range(2):
             load_v(j, v_planes[j])
         load_xm(1)
-        load_v(3, v_planes[3])
-        v_windows = [placed([P, T], F32, "v_window%d" % j, PLANE_KIB * j) for j in range(BLOCKS)]
+        load_v(1, v_windows[1])
+        for j in range(2, BLOCKS):
+            load_v(j, v_planes[j])
         load_v(3, v_windows[3])
 
         w_grouped = held([P, N, PACK], BF16, "w_grouped")
@@ -224,12 +226,14 @@ def tile_attend_ghub_ada_kernel(tc, xT, wT, y, wt, xm, vT, offs, out_0, out_1):
             return dw
 
         def gather_v(j):
-            nv = held([P, N], F32, "nv%d" % j, "nv1" if j == 3 else None)
-            nc.scalar.activation(out=nv[:], in_=v_planes[j][:].indirect(offsets[:]), func=ACT.Copy)
+            nv = held([P, N], F32, "nv%d" % j, "g_grouped1" if j == 0 else None)
+            nc.vector.tensor_copy(out=nv[:], in_=v_planes[j][:].indirect(offsets[:]))
             return nv
 
         def copy_v(j):
-            nc.vector.tensor_copy(out=v_windows[j][:], in_=v_planes[j][:])
+            for h in range(2):
+                half = slice(h * T // 2, (h + 1) * T // 2)
+                nc.scalar.activation(out=v_windows[j][:, half], in_=v_planes[j][:, half], func=ACT.Copy)
 
         def add_square(j, dw, nv):
             square = held([P, N], F32, "square%d" % j)
@@ -238,12 +242,13 @@ def tile_attend_ghub_ada_kernel(tc, xT, wT, y, wt, xm, vT, offs, out_0, out_1):
             adder.tensor_tensor(out=nv[:], in0=nv[:], in1=square[:], op=ALU.add)
 
         def roots(j, nv):
-            root = held([P, N], F32, "root%d" % j, "v3" if j == 2 else None)
+            root = held([P, N], F32, "root%d" % j)
             shifted = held([P, N], F32, "shifted%d" % j)
             factor = held([P, N], F32, "factor%d" % j, "shifted%d" % (j - 1) if j % 2 else "square%d" % (j + 1))
-            for half in halves:
+            quarters = [slice(q * N // 4, (q + 1) * N // 4) for q in range(4)]
+            for half in quarters:
                 nc.scalar.activation(out=root[:, half], in_=nv[:, half], func=ACT.Abs_reciprocal_sqrt, bias=guard[:])
-            for half in halves:
+            for half in quarters:
                 nc.scalar.activation(out=shifted[:, half], in_=root[:, half], func=ACT.Abs_reciprocal_sqrt,
                                      scale=EPS, bias=one[:])
             nc.gpsimd.tensor_tensor(out=factor[:], in0=root[:], in1=shifted[:], op=ALU.mult)
@@ -260,7 +265,7 @@ def tile_attend_ghub_ada_kernel(tc, xT, wT, y, wt, xm, vT, offs, out_0, out_1):
             nc.sync.dma_start(out=out_1[j * P:(j + 1) * P, :], in_=v_windows[j][:])
 
         def put_step(j, dw, factor):
-            step = held([P, N], F32, "step%d" % j, "xm_grouped2")
+            step = held([P, N], F32, "step%d" % j, "v3" if j else "xm_grouped2")
             nc.vector.scalar_tensor_tensor(out=step[:], in0=dw[:], scalar=-LR, in1=factor[:],
                                            op0=ALU.mult, op1=ALU.mult)
             nc.vector.tensor_copy(out=step_windows[j % 2][:].indirect(offsets[:]), in_=step[:])
@@ -274,24 +279,23 @@ def tile_attend_ghub_ada_kernel(tc, xT, wT, y, wt, xm, vT, offs, out_0, out_1):
         xm_quant = quantize_xm(0, 1, interleave_xm(0, 1, "clipped0", False))
         xm_quant.extend(quantize_xm(1, 1, interleave_xm(1, 1, None, False)))
         products = [second_product(xm_quant[j]) for j in range(2)]
-        picked = []
+        picked = [gather_v(j) for j in range(2)]
+        copy_v(0)
         for j in range(2):
-            picked.append(gather_v(j))
-            copy_v(j)
             add_square(j, products[j], picked[j])
-        factors = [roots(j, picked[j]) for j in range(2)]
+        factors = [roots(0, picked[0])]
         put_squares(0, picked[0])
-        copy_v(2)
-        picked.append(gather_v(2))
-        put_squares(1, picked[1])
-        xm_quant.extend(quantize_xm(2, 2, interleave_xm(2, 2, None, True)))
+        xm_quant.extend(quantize_xm(2, 2, interleave_xm(2, 2, None, False)))
         products.extend(second_product(xm_quant[j]) for j in range(2, BLOCKS))
-        picked.append(gather_v(3))
+        factors.append(roots(1, picked[1]))
+        put_squares(1, picked[1])
+        picked.extend(gather_v(j) for j in range(2, BLOCKS))
         for j in range(2):
             put_step(j, products[j], factors[j])
         for j in range(2, BLOCKS):
             add_square(j, products[j], picked[j])
         factors.extend(roots(j, picked[j]) for j in range(2, BLOCKS))
+        copy_v(2)
         for j in range(2, BLOCKS):
             put_squares(j, picked[j])
             put_step(j, products[j], factors[j])

@@ -238,8 +238,13 @@ def tile_attend_ghub_ada_kernel(tc, xT, wT, y, wt, xm, vT, offs, out_0, out_1):
         def add_square(j, dw, nv):
             square = held([P, N], F32, "square%d" % j)
             nc.scalar.activation(out=square[:], in_=dw[:], func=ACT.Square)
+            if nv is None:
+                nv = held([P, N], F32, "nv%d" % j)
+                nc.vector.tensor_tensor(out=nv[:], in0=v_planes[j][:].indirect(offsets[:]), in1=square[:], op=ALU.add)
+                return nv
             adder = nc.vector if j == 0 else nc.gpsimd
             adder.tensor_tensor(out=nv[:], in0=nv[:], in1=square[:], op=ALU.add)
+            return nv
 
         def roots(j, nv):
             root = held([P, N], F32, "root%d" % j)
@@ -289,11 +294,9 @@ def tile_attend_ghub_ada_kernel(tc, xT, wT, y, wt, xm, vT, offs, out_0, out_1):
         products.extend(second_product(xm_quant[j]) for j in range(2, BLOCKS))
         factors.append(roots(1, picked[1]))
         put_squares(1, picked[1])
-        picked.extend(gather_v(j) for j in range(2, BLOCKS))
-        for j in range(2):
-            put_step(j, products[j], factors[j])
-        for j in range(2, BLOCKS):
-            add_square(j, products[j], picked[j])
+        put_step(0, products[0], factors[0])
+        picked.extend(add_square(j, products[j], None) for j in range(2, BLOCKS))
+        put_step(1, products[1], factors[1])
         factors.extend(roots(j, picked[j]) for j in range(2, BLOCKS))
         copy_v(2)
         for j in range(2, BLOCKS):

@@ -242,8 +242,7 @@ def tile_attend_ghub_ada_kernel(tc, xT, wT, y, wt, xm, vT, offs, out_0, out_1):
                 nv = held([P, N], F32, "nv%d" % j)
                 nc.vector.tensor_tensor(out=nv[:], in0=v_planes[j][:].indirect(offsets[:]), in1=square[:], op=ALU.add)
                 return nv
-            adder = nc.vector if j == 0 else nc.gpsimd
-            adder.tensor_tensor(out=nv[:], in0=nv[:], in1=square[:], op=ALU.add)
+            nc.gpsimd.tensor_tensor(out=nv[:], in0=nv[:], in1=square[:], op=ALU.add)
             return nv
 
         def roots(j, nv):
@@ -270,7 +269,7 @@ def tile_attend_ghub_ada_kernel(tc, xT, wT, y, wt, xm, vT, offs, out_0, out_1):
             nc.sync.dma_start(out=out_1[j * P:(j + 1) * P, :], in_=v_windows[j][:])
 
         def put_step(j, dw, factor):
-            step = held([P, N], F32, "step%d" % j, "v3" if j else "xm_grouped2")
+            step = held([P, N], F32, "step%d" % j, ("xm_raw1_1", "v3", None, "step2")[j])
             nc.vector.scalar_tensor_tensor(out=step[:], in0=dw[:], scalar=-LR, in1=factor[:],
                                            op0=ALU.mult, op1=ALU.mult)
             nc.vector.tensor_copy(out=step_windows[j % 2][:].indirect(offsets[:]), in_=step[:])
@@ -285,9 +284,9 @@ def tile_attend_ghub_ada_kernel(tc, xT, wT, y, wt, xm, vT, offs, out_0, out_1):
         xm_quant.extend(quantize_xm(1, 1, interleave_xm(1, 1, None, False)))
         products = [second_product(xm_quant[j]) for j in range(2)]
         picked = [gather_v(j) for j in range(2)]
+        add_square(0, products[0], picked[0])
         copy_v(0)
-        for j in range(2):
-            add_square(j, products[j], picked[j])
+        add_square(1, products[1], picked[1])
         factors = [roots(0, picked[0])]
         put_squares(0, picked[0])
         xm_quant.extend(quantize_xm(2, 2, interleave_xm(2, 2, None, False)))

@@ -210,9 +210,15 @@ def tile_attend_ghub_ada_kernel(tc, xT, wT, y, wt, xm, vT, offs, out_0, out_1):
         def quantize_xm(first, count, grouped):
             codes = held([P, count, ROW_PASSES * P], U32, "xm_codes%d" % first)
             scales = held([P, count, ROW_PASSES * P], U8, "xm_scales%d" % first)
-            nc.vector.quantize_mx(out=codes[:].rearrange("p b c -> p (b c)").bitcast(E4M3),
-                                  scales=scales[:].rearrange("p b c -> p (b c)"),
-                                  in_=grouped[:].rearrange("p b g d t -> p (b g d t)"))
+            if first == 0:
+                for g in range(ROW_PASSES):
+                    cols = slice(g * P, (g + 1) * P)
+                    nc.vector.quantize_mx(out=codes[:, 0, cols].bitcast(E4M3), scales=scales[:, 0, cols],
+                                          in_=grouped[:, 0, g].rearrange("p d t -> p (d t)"))
+            else:
+                nc.vector.quantize_mx(out=codes[:].rearrange("p b c -> p (b c)").bitcast(E4M3),
+                                      scales=scales[:].rearrange("p b c -> p (b c)"),
+                                      in_=grouped[:].rearrange("p b g d t -> p (b g d t)"))
             return [(codes[:, b, :], scales[:, b, :]) for b in range(count)]
 
         def second_product(xm_quant):

@@ -110,6 +110,7 @@ def tile_attend_ghub_ada_kernel(tc, xT, wT, y, wt, xm, vT, offs, out_0, out_1):
         for j in range(2, BLOCKS):
             load_v(j, v_planes[j])
         load_v(3, v_windows[3])
+        nc.sync.dma_start(out=v_windows[2][:, T // 2:], in_=vT[2 * P:3 * P, T // 2:])
 
         w_grouped = held([P, N, PACK], BF16, "w_grouped")
         w_codes = held([P, N], U32, "w_codes")
@@ -237,7 +238,7 @@ def tile_attend_ghub_ada_kernel(tc, xT, wT, y, wt, xm, vT, offs, out_0, out_1):
             return nv
 
         def copy_v(j):
-            for h in range(2):
+            for h in range(1 if j == 2 else 2):
                 half = slice(h * T // 2, (h + 1) * T // 2)
                 nc.scalar.activation(out=v_windows[j][:, half], in_=v_planes[j][:, half], func=ACT.Copy)
 
@@ -272,7 +273,8 @@ def tile_attend_ghub_ada_kernel(tc, xT, wT, y, wt, xm, vT, offs, out_0, out_1):
                 for h in range(2):
                     nc.scalar.activation(out=v_windows[j][:].indirect(half_lists[h]), in_=nv[:, halves[h]],
                                          func=ACT.Copy)
-            nc.sync.dma_start(out=out_1[j * P:(j + 1) * P, :], in_=v_windows[j][:])
+            queue = nc.scalar if j == 2 else nc.sync
+            queue.dma_start(out=out_1[j * P:(j + 1) * P, :], in_=v_windows[j][:])
 
         def put_step(j, dw, factor):
             step = held([P, N], F32, "step%d" % j, ("xm_raw1_1", "v3", None, "step2")[j])

@@ -277,9 +277,14 @@ def tile_attend_ghub_ada_kernel(tc, xT, wT, y, wt, xm, vT, offs, out_0, out_1):
             queue.dma_start(out=out_1[j * P:(j + 1) * P, :], in_=v_windows[j][:])
 
         def put_step(j, dw, factor):
-            step = held([P, N], F32, "step%d" % j, ("xm_raw1_1", "v3", None, "step2")[j])
-            nc.vector.scalar_tensor_tensor(out=step[:], in0=dw[:], scalar=-LR, in1=factor[:],
-                                           op0=ALU.mult, op1=ALU.mult)
+            step = held([P, N], F32, "step%d" % j, ("xm_raw1_1", "v3", None, "square3")[j])
+            if j == BLOCKS - 1:
+                scaled = held([P, N], F32, "scaled")
+                nc.scalar.activation(out=scaled[:], in_=dw[:], func=ACT.Copy, scale=-LR)
+                nc.gpsimd.tensor_tensor(out=step[:], in0=scaled[:], in1=factor[:], op=ALU.mult)
+            else:
+                nc.vector.scalar_tensor_tensor(out=step[:], in0=dw[:], scalar=-LR, in1=factor[:],
+                                               op0=ALU.mult, op1=ALU.mult)
             nc.vector.tensor_copy(out=step_windows[j % 2][:].indirect(offsets[:]), in_=step[:])
             nc.sync.dma_start(out=out_0[j * P:(j + 1) * P, :], in_=step_windows[j % 2][:])
 

from contextlib import ExitStack

import concourse.mybir as mybir

N, T, D, R = 512, 2048, 512, 1024
LR = 0.1
EPS = 0.001
FLOPS = 2 * 2 * D * R * N

F32 = mybir.dt.float32
BF16 = mybir.dt.bfloat16
U32 = mybir.dt.uint32
U16 = mybir.dt.uint16
U8 = mybir.dt.uint8
E4M3 = mybir.dt.float8_e4m3fn_x4
E5M2 = mybir.dt.float8_e5m2_x4
ALU = mybir.AluOpType
ACT = mybir.ActivationFunctionType

P = 128
PACK = 4
K_PASS = P * PACK
ROW_PASSES = R // K_PASS
BLOCKS = D // P
RUN = 4
CLIPS_ON_GPSIMD = (4, 2)
X_PIECES = ((0, 256), (256, 512))
X_ON_VECTOR = (44, 64)
PLANE_KIB = 8
Y1_AT = PLANE_KIB * PACK


def tile_attend_ghub_ada_kernel(tc, xT, wT, y, wt, xm, vT, offs, out_0, out_1):
    nc = tc.nc
    with ExitStack() as ctx:
        keep = ctx.enter_context(tc.tile_pool(name="keep", bufs=1))
        handed = ctx.enter_context(tc.tile_pool(name="handed", bufs=1))
        psum = ctx.enter_context(tc.psum_pool(name="psum", bufs=4))

        def held(shape, dtype, name, slot=None):
            return keep.tile(shape, dtype, name=name, tag=slot or name, align_bytes=64)

        def placed(shape, dtype, name, kib):
            return handed.tile(shape, dtype, name=name, offset=kib * 1024, align_bytes=64)

        big = held([P, 1], F32, "big")
        guard = held([P, 1], F32, "guard")
        one = held([P, 1], F32, "one")
        nc.vector.memset(big[:], 2.0 ** 80)
        nc.scalar.activation(out=big[:], in_=big[:], func=ACT.Abs_reciprocal_sqrt)
        nc.scalar.activation(out=guard[:], in_=big[:], func=ACT.Square)
        nc.vector.memset(one[:], 1.0)

        step_windows = [held([P, T], F32, "step_window%d" % j) for j in range(2)]
        for j in range(2):
            nc.vector.memset(step_windows[j][:], 0.0)

        offsets = keep.tile([P, N // 16], U16, name="offsets")
        w_planes = [placed([P, T], F32, "w%d" % j, PLANE_KIB * j) for j in range(PACK)]
        w_rows = wT.rearrange("(p j) c -> p j c", j=PACK)
        weight = held([P, ROW_PASSES, PACK], F32, "weight")
        x_raw = [[held([P, PACK, hi - lo], F32, "x_raw%d_%d" % (g, lo)) for lo, hi in X_PIECES]
                 for g in range(ROW_PASSES)]
        y0 = held([P, PACK, N], F32, "y0")
        y1_head = placed([P, PACK - 1, N], F32, "y1_head", Y1_AT)
        y1_last = held([P, N], F32, "y1_last")
        y_t = [[y0[:, t, :] for t in range(PACK)], [y1_head[:, t, :] for t in range(PACK - 1)] + [y1_last[:]]]
        y1_raw = [held([P, N], F32, "y1_raw%d" % t) for t in range(PACK)]
        x_rows = xT[0].rearrange("(p j) r -> p j r", j=PACK)
        y_rows = y[0].rearrange("(g p t) i -> g p t i", g=ROW_PASSES, t=PACK)
        xm_rows = xm[0].rearrange("(g p t) d -> g p t d", g=ROW_PASSES, t=PACK)
        xm_raw = [[held([P, PACK, 2 * P], F32, "xm_raw%d_%d" % (h, g)) for g in range(ROW_PASSES)] for h in range(2)]
        v_planes = [held([P, T], F32, "v%d" % j) for j in range(BLOCKS)]

        nc.sync.dma_start(out=w_planes[0][:], in_=w_rows[:, 0, :])
        nc.sync.dma_start(offsets[:], offs)
        for j in range(1, PACK):
            nc.sync.dma_start(out=w_planes[j][:], in_=w_rows[:, j, :])
        nc.scalar.dma_start(out=weight[:], in_=wt[0].rearrange("(g p t) o -> p g (t o)", g=ROW_PASSES, t=PACK))

        def load_x(g, h):
            lo, hi = X_PIECES[h]
            nc.sync.dma_start(out=x_raw[g][h][:], in_=x_rows[:, :, g * K_PASS + lo:g * K_PASS + hi])

        def load_y(g, t):
            nc.sync.dma_start(out=y0[:, t, :] if g == 0 else y1_raw[t][:], in_=y_rows[g, :, t, :])

        def load_xm(h):
            for g in range(ROW_PASSES):
                nc.sync.dma_start(out=xm_raw[h][g][:], in_=xm_rows[g, :, :, 2 * h * P:2 * (h + 1) * P])

        def load_v(j, tile):
            nc.sync.dma_start(out=tile[:], in_=vT[j * P:(j + 1) * P, :])

        load_x(0, 0)
        load_x(0, 1)
        for h in range(2):
            load_y(0, h)
            load_x(1, h)
        for t in range(2, PACK):
            load_y(0, t)
        for t in range(PACK):
            load_y(1, t)
        load_xm(0)
        v_windows = [placed([P, T], F32, "v_window%d" % j, PLANE_KIB * j) for j in range(BLOCKS)]
        for j in range(2):
            load_v(j, v_planes[j])
        load_xm(1)
        load_v(1, v_windows[1])
        for j in range(2, BLOCKS):
            load_v(j, v_planes[j])
        load_v(3, v_windows[3])
        nc.sync.dma_start(out=v_windows[2][:, T // 2:], in_=vT[2 * P:3 * P, T // 2:])

        w_grouped = held([P, N, PACK], BF16, "w_grouped")
        w_codes = held([P, N], U32, "w_codes")
        w_scales = held([P, N], U8, "w_scales")
        halves = [slice(h * N // 2, (h + 1) * N // 2) for h in range(2)]
        half_lists = [offsets[:, h * N // 32:(h + 1) * N // 32] for h in range(2)]
        for j in range(PACK - 1):
            nc.vector.tensor_copy(out=w_grouped[:, :, j], in_=w_planes[j][:].indirect(offsets[:]))
        for h in range(2):
            nc.vector.tensor_copy(out=w_grouped[:, halves[h], PACK - 1],
                                  in_=w_planes[PACK - 1][:].indirect(half_lists[h]))
        for h in range(2):
            nc.vector.quantize_mx(out=w_codes[:, halves[h]].bitcast(E4M3), scales=w_scales[:, halves[h]],
                                  in_=w_grouped[:, halves[h], :].rearrange("p n j -> p (n j)"))

        neg_weight = held([P, ROW_PASSES, PACK], F32, "neg_weight")
        upper = held([P, ROW_PASSES, PACK], F32, "upper")
        lower = held([P, ROW_PASSES, PACK], F32, "lower")
        nc.vector.tensor_scalar(out=neg_weight[:], in0=weight[:], scalar1=-1.0, scalar2=None, op0=ALU.mult)
        nc.vector.tensor_tensor(out=upper[:], in0=weight[:], in1=neg_weight[:], op=ALU.max)
        nc.vector.tensor_tensor(out=lower[:], in0=weight[:], in1=neg_weight[:], op=ALU.min)

        def quantize_x(g):
            x_grouped = held([P, K_PASS, PACK], BF16, "x_grouped%d" % g)
            dst = x_grouped[:].rearrange("p (t m) j -> p m j t", t=PACK)
            for h, (lo, hi) in enumerate(X_PIECES):
                src = x_raw[g][h][:].rearrange("p j (m t) -> p m j t", t=PACK)
                split = X_ON_VECTOR[g] if h == 1 else 0
                if split > 0:
                    nc.vector.tensor_copy(out=dst[:, lo // PACK:lo // PACK + split], in_=src[:, :split])
                if split < (hi - lo) // PACK:
                    nc.scalar.copy(out=dst[:, lo // PACK + split:hi // PACK], in_=src[:, split:])
            x_codes = held([P, K_PASS], U32, "x_codes%d" % g)
            x_scales = held([P, K_PASS], U8, "x_scales%d" % g)
            for cols in (slice(0, P), slice(P, 2 * P), slice(2 * P, 4 * P)):
                nc.vector.quantize_mx(out=x_codes[:, cols].bitcast(E4M3), scales=x_scales[:, cols],
                                      in_=x_grouped[:, cols, :].rearrange("p c j -> p (c j)"))
            return x_codes, x_scales

        def first_product(g, x_quant):
            x_codes, x_scales = x_quant
            banks = []
            for t in range(PACK):
                raw = y_t[g][t] if g == 0 else y1_raw[t][:]
                nc.scalar.activation(out=y_t[g][t], in_=raw, func=ACT.Copy, scale=weight[:, g, t:t + 1])
                acc = psum.tile([P, N], F32, name="acc")
                cols = slice(t * P, (t + 1) * P)
                nc.tensor.matmul_mx(out=acc[:], lhsT=x_codes[:, cols].bitcast(E4M3), lhsT_scale=x_scales[:, cols],
                                    rhs=w_codes[:].bitcast(E4M3), rhs_scale=w_scales[:], start=True, stop=True)
                banks.append(acc)
            return banks

        def clip(g, banks):
            if g == 0:
                clipped = held([P, PACK, N], BF16, "clipped0")
            else:
                clipped = held([P, PACK, N], BF16, "clipped1")
            for t in range(PACK):
                nc.vector.scalar_tensor_tensor(out=y_t[g][t], in0=banks[t][:], scalar=weight[:, g, t:t + 1],
                                               in1=y_t[g][t], op0=ALU.mult, op1=ALU.subtract)
            for t in range(PACK):
                engine = nc.gpsimd if t < CLIPS_ON_GPSIMD[g] else nc.vector
                engine.tensor_scalar(out=clipped[:, t, :], in0=y_t[g][t], scalar1=upper[:, g, t:t + 1],
                                     scalar2=lower[:, g, t:t + 1], op0=ALU.min, op1=ALU.max)
            return clipped

        def interleave_g(g, clipped):
            g_grouped = held([P, N, PACK], BF16, "g_grouped%d" % g, "y1_raw3" if g == 0 else None)
            dst = g_grouped[:].rearrange("p (c i) t -> p c t i", i=RUN)
            src = clipped[:].rearrange("p t (c i) -> p c t i", i=RUN)
            if g == 0:
                nc.scalar.copy(out=dst, in_=src)
            else:
                nc.vector.tensor_copy(out=dst, in_=src)
            return g_grouped

        def quantize_g(g, g_grouped):
            codes = placed([P, N], U32, "g_codes0", Y1_AT + 2) if g == 0 else held([P, N], U32, "g_codes1")
            scales = held([P, N], U8, "g_scales%d" % g)
            nc.vector.quantize_mx(out=codes[:].bitcast(E5M2), scales=scales[:],
                                  in_=g_grouped[:].rearrange("p n t -> p (n t)"))
            return codes, scales

        def interleave_xm(first, count, slot, on_vector):
            grouped = held([P, count, ROW_PASSES, P, PACK], BF16, "xm_grouped%d" % first, slot)
            for g in range(ROW_PASSES):
                for b in range(count):
                    j = first + b
                    raw = xm_raw[j // 2][g][:, :, (j % 2) * P:(j % 2 + 1) * P]
                    dst = grouped[:, b, g].rearrange("p (c i) t -> p c t i", i=RUN)
                    src = raw.rearrange("p t (c i) -> p c t i", i=RUN)
                    if on_vector:
                        nc.vector.tensor_copy(out=dst, in_=src)
                    else:
                        nc.scalar.copy(out=dst, in_=src)
            return grouped

        def quantize_xm(first, count, grouped):
            codes = held([P, count, ROW_PASSES * P], U32, "xm_codes%d" % first)
            scales = held([P, count, ROW_PASSES * P], U8, "xm_scales%d" % first)
            if first == 0:
                for g in range(ROW_PASSES):
                    cols = slice(g * P, (g + 1) * P)
                    nc.vector.quantize_mx(out=codes[:, 0, cols].bitcast(E4M3), scales=scales[:, 0, cols],
                                          in_=grouped[:, 0, g].rearrange("p d t -> p (d t)"))
            else:
                nc.vector.quantize_mx(out=codes[:].rearrange("p b c -> p (b c)").bitcast(E4M3),
                                      scales=scales[:].rearrange("p b c -> p (b c)"),
                                      in_=grouped[:].rearrange("p b g d t -> p (b g d t)"))
            return [(codes[:, b, :], scales[:, b, :]) for b in range(count)]

        def second_product(xm_quant):
            xm_codes, xm_scales = xm_quant
            dw = psum.tile([P, N], F32, name="dw")
            for g in range(ROW_PASSES):
                cols = slice(g * P, (g + 1) * P)
                nc.tensor.matmul_mx(out=dw[:], lhsT=xm_codes[:, cols].bitcast(E4M3), lhsT_scale=xm_scales[:, cols],
                                    rhs=g_quant[g][0][:].bitcast(E5M2), rhs_scale=g_quant[g][1][:],
                                    start=(g == 0), stop=(g == ROW_PASSES - 1))
            return dw

        def gather_v(j):
            nv = held([P, N], F32, "nv%d" % j, "g_grouped1" if j == 0 else None)
            nc.vector.tensor_copy(out=nv[:], in_=v_planes[j][:].indirect(offsets[:]))
            return nv

        def copy_v(j):
            for h in range(1 if j == 2 else 2):
                half = slice(h * T // 2, (h + 1) * T // 2)
                nc.scalar.activation(out=v_windows[j][:, half], in_=v_planes[j][:, half], func=ACT.Copy)

        def add_square(j, dw, nv):
            square = held([P, N], F32, "square%d" % j)
            nc.scalar.activation(out=square[:], in_=dw[:], func=ACT.Square)
            if nv is None:
                nv = held([P, N], F32, "nv%d" % j)
                nc.vector.tensor_tensor(out=nv[:], in0=v_planes[j][:].indirect(offsets[:]), in1=square[:], op=ALU.add)
                return nv
            nc.gpsimd.tensor_tensor(out=nv[:], in0=nv[:], in1=square[:], op=ALU.add)
            return nv

        def roots(j, nv):
            root = held([P, N], F32, "root%d" % j)
            shifted = held([P, N], F32, "shifted%d" % j)
            factor = held([P, N], F32, "factor%d" % j, "shifted%d" % (j - 1) if j % 2 else "square%d" % (j + 1))
            quarters = [slice(q * N // 4, (q + 1) * N // 4) for q in range(4)]
            for half in quarters:
                nc.scalar.activation(out=root[:, half], in_=nv[:, half], func=ACT.Abs_reciprocal_sqrt, bias=guard[:])
            for half in quarters:
                nc.scalar.activation(out=shifted[:, half], in_=root[:, half], func=ACT.Abs_reciprocal_sqrt,
                                     scale=EPS, bias=one[:])
            nc.gpsimd.tensor_tensor(out=factor[:], in0=root[:], in1=shifted[:], op=ALU.mult)
            nc.gpsimd.tensor_tensor(out=factor[:], in0=factor[:], in1=shifted[:], op=ALU.mult)
            return factor

        def put_squares(j, nv):
            if j == 0:
                nc.vector.tensor_copy(out=v_windows[j][:].indirect(offsets[:]), in_=nv[:])
            else:
                for h in range(2):
                    nc.scalar.activation(out=v_windows[j][:].indirect(half_lists[h]), in_=nv[:, halves[h]],
                                         func=ACT.Copy)
            queue = nc.scalar if j == 2 else nc.sync
            queue.dma_start(out=out_1[j * P:(j + 1) * P, :], in_=v_windows[j][:])

        def put_step(j, dw, factor):
            step = held([P, N], F32, "step%d" % j, ("xm_raw1_1", "v3", None, "square3")[j])
            if j == BLOCKS - 1:
                scaled = held([P, N], F32, "scaled")
                nc.scalar.activation(out=scaled[:], in_=dw[:], func=ACT.Copy, scale=-LR)
                nc.gpsimd.tensor_tensor(out=step[:], in0=scaled[:], in1=factor[:], op=ALU.mult)
            else:
                nc.vector.scalar_tensor_tensor(out=step[:], in0=dw[:], scalar=-LR, in1=factor[:],
                                               op0=ALU.mult, op1=ALU.mult)
            nc.vector.tensor_copy(out=step_windows[j % 2][:].indirect(offsets[:]), in_=step[:])
            nc.sync.dma_start(out=out_0[j * P:(j + 1) * P, :], in_=step_windows[j % 2][:])

        x_quant = [quantize_x(g) for g in range(ROW_PASSES)]
        clipped0 = clip(0, first_product(0, x_quant[0]))
        clipped1 = clip(1, first_product(1, x_quant[1]))
        g_grouped = [interleave_g(0, clipped0), interleave_g(1, clipped1)]
        g_quant = [quantize_g(g, g_grouped[g]) for g in range(ROW_PASSES)]
        xm_quant = quantize_xm(0, 1, interleave_xm(0, 1, "clipped0", False))
        xm_quant.extend(quantize_xm(1, 1, interleave_xm(1, 1, None, False)))
        products = [second_product(xm_quant[j]) for j in range(2)]
        picked = [gather_v(j) for j in range(2)]
        add_square(0, products[0], picked[0])
        copy_v(0)
        add_square(1, products[1], picked[1])
        factors = [roots(0, picked[0])]
        put_squares(0, picked[0])
        xm_quant.extend(quantize_xm(2, 2, interleave_xm(2, 2, None, False)))
        products.extend(second_product(xm_quant[j]) for j in range(2, BLOCKS))
        factors.append(roots(1, picked[1]))
        put_squares(1, picked[1])
        put_step(0, products[0], factors[0])
        picked.extend(add_square(j, products[j], None) for j in range(2, BLOCKS))
        put_step(1, products[1], factors[1])
        factors.extend(roots(j, picked[j]) for j in range(2, BLOCKS))
        copy_v(2)
        for j in range(2, BLOCKS):
            put_squares(j, picked[j])
            put_step(j, products[j], factors[j])
